import numpy as np
import ml_dtypes


def mxq(x, axis, fmt="e4m3"):
    dtype, down = {"e4m3": (ml_dtypes.float8_e4m3fn, 7), "e5m2": (ml_dtypes.float8_e5m2, 14)}[fmt]
    v = np.moveaxis(np.asarray(x, np.float32).astype(ml_dtypes.bfloat16).astype(np.float64), axis, -1)
    blocks = v.reshape(v.shape[:-1] + (-1, 32))
    amax = np.abs(blocks).max(-1, keepdims=True)
    byte = np.maximum(np.where(amax > 0, np.frexp(amax)[1] - 1 + 127, 0) - down, 1)
    scale = np.exp2(byte - 127.0)
    codes = (blocks / scale).astype(np.float32).astype(dtype).astype(np.float64)
    return np.moveaxis((codes * scale).reshape(v.shape), -1, axis)


WIDE = False


def mx_kscale(k):
    if not WIDE:
        return np.ones(k)
    levels = np.array([10, -10, 5, -5, 0])
    if k % 512:
        return np.exp2(np.random.permutation(np.resize(levels, k // 32))).repeat(32)
    a = np.empty((k // 512, 16))
    for p in range(k // 512):
        a[p, :8] = np.random.permutation(np.resize(levels, 8))
        for g in range(8):
            far = levels[np.abs(levels - a[p, g]) >= 10]
            a[p, g + 8] = far[np.random.randint(len(far))]
    return np.exp2(a.ravel()).repeat(32)


BF16 = ml_dtypes.bfloat16


def bf(x):
    return np.asarray(x, np.float32).astype(BF16)


def f64(x):
    return np.asarray(x).astype(np.float64)


E2M1 = np.array([0.0, 0.5, 1.0, 1.5, 2.0, 3.0, 4.0, 6.0, -0.0, -0.5, -1.0, -1.5, -2.0, -3.0, -4.0, -6.0])


def pack_weight(w, fmt):
    k, n = w.shape
    w = f64(bf(w)).reshape(k // 32, 32, n)
    amax = np.abs(w).max(1)
    if fmt == "e4m3":
        byte = np.frexp(amax)[1] - 1 + 127 - 7
    else:
        mant, ex = np.frexp(amax / 6.0)
        byte = np.where(mant > 0.5, ex, ex - 1) + 127
    byte = np.clip(np.where(amax > 0, byte, 1), 1, 254)
    scaled = (w * np.exp2(127.0 - byte)[:, None, :]).reshape(k, n).astype(np.float32)
    by_word = np.ascontiguousarray(scaled.reshape(k // 512, 128, 4, n).transpose(0, 1, 3, 2))
    if fmt == "e4m3":
        words = by_word.astype(ml_dtypes.float8_e4m3fn).view(np.uint8)
    else:
        c = by_word.astype(ml_dtypes.float4_e2m1fn).view(np.uint8) & 0xF
        words = c[..., 0::2] | (c[..., 1::2] << 4)
    return np.ascontiguousarray(words), np.ascontiguousarray(byte.astype(np.uint8).reshape(k // 512, 16, n))


def unpack_weight(words, scales, fmt):
    g, p, n, _ = words.shape
    if fmt == "e4m3":
        vals = np.ascontiguousarray(words).view(ml_dtypes.float8_e4m3fn).astype(np.float64)
    else:
        nib = np.empty((g, p, n, 4), np.uint8)
        nib[..., 0::2] = words & 0xF
        nib[..., 1::2] = words >> 4
        vals = E2M1[nib]
    vals = vals * np.repeat(np.exp2(scales.astype(np.float64) - 127.0), 8, axis=1)[..., None]
    return vals.transpose(0, 1, 3, 2).reshape(g * 512, n)
def pack4(w):
    words, scales = pack_weight(w, "e2m1")
    return words.reshape(words.shape[0], 128, -1), scales


def unpack4(words, scales):
    return unpack_weight(words.reshape(words.shape[0], 128, -1, 2), scales, "e2m1")


def planes(Y):
    n, m = Y.shape
    b = f64(bf(Y)).reshape(n // 32, 32, m)
    amax = np.abs(b).max(1)
    byte = np.clip(np.where(amax > 0, np.frexp(amax)[1] - 1 + 127 - 7, 1), 1, 254)
    codes = (b * np.exp2(127.0 - byte)[:, None, :]).reshape(n, m).astype(np.float32).astype(ml_dtypes.float8_e4m3fn).view(np.uint8)
    words = codes.reshape(n // 512, 128, 4, m).transpose(0, 1, 3, 2)
    return np.ascontiguousarray(words), np.ascontiguousarray(byte.astype(np.uint8).reshape(n // 512, 16, m))


B, S, D, F = 4, 512, 512, 1024


def erf(a):
    c = np.clip(a, -6.0, 6.0)
    c2 = 2.0 * c * c
    term = c
    total = c
    for n in range(1, 150):
        term = term * c2 / (2.0 * n + 1.0)
        total = total + term
    return np.where(np.abs(a) <= 6.0, 2.0 / np.sqrt(np.pi) * np.exp(-c * c) * total, np.sign(a))


def gelu_erf(h):
    return 0.5 * h * (1.0 + erf(h / np.sqrt(2.0)))


def setup_inputs():
    s = mx_kscale(S)
    r = mx_kscale(D)
    x = bf(np.random.standard_normal((B, S, D)))
    gt = bf((1.0 + 0.1 * np.random.standard_normal(S)) * s)
    t = np.random.standard_normal((S, S)) / np.sqrt(S) / s[None, :]
    t_words, t_scales = pack4(np.ascontiguousarray(t.T))
    ls = bf(np.random.uniform(0.5, 1.5, D))
    a2 = bf((1.0 + 0.1 * np.random.standard_normal(D)) * r)
    b2 = bf(0.3 * np.random.standard_normal(D) * r)
    w_words, w_scales = pack4(np.random.standard_normal((D, F)) / np.sqrt(D) / r[:, None])
    return {
        "x": x,
        "gt": gt,
        "t_words": t_words,
        "t_scales": t_scales,
        "ls": ls,
        "a2": a2,
        "b2": b2,
        "w_words": w_words,
        "w_scales": w_scales,
    }


def core(x, gt, t_words, t_scales, ls, a2, b2, w_words, w_scales):
    x, gt, ls, a2, b2 = f64(x), f64(gt), f64(ls), f64(a2), f64(b2)
    n = gt[None, :, None] * x
    m = unpack4(t_words, t_scales).T @ mxq(n, 1, "e4m3")
    z = x + ls[None, None, :] * m
    u = a2[None, None, :] * z + b2[None, None, :]
    h = mxq(u, 2, "e4m3") @ unpack4(w_words, w_scales)
    return gelu_erf(h)


def reference(x, gt, t_words, t_scales, ls, a2, b2, w_words, w_scales):
    R_out = core(x, gt, t_words, t_scales, ls, a2, b2, w_words, w_scales)
    words, scales = planes(np.moveaxis(R_out, 2, 0).reshape(1024, -1))
    return R_out, words, scales

@@ -1,0 +1,457 @@
+from contextlib import ExitStack
+
+import concourse.mybir as mybir
+from concourse.masks import make_identity
+
+B, S, D, F = 4, 512, 512, 1024
+FLOPS = 2 * B * S * S * D + 2 * B * S * D * F
+
+F32 = mybir.dt.float32
+BF16 = mybir.dt.bfloat16
+I32 = mybir.dt.int32
+U32 = mybir.dt.uint32
+U8 = mybir.dt.uint8
+FP8X4 = mybir.dt.float8_e4m3fn_x4
+FP4X4 = mybir.dt.float4_e2m1fn_x4
+ACT = mybir.ActivationFunctionType
+ALU = mybir.AluOpType
+
+P = 128
+WB = 4
+POS = {1: [0, 0, 1, 3], 2: [0, 4, 4, 4, 7, 8], 3: [0, 6, 6, 6, 7, 10]}
+YENG = {(1, 0): "scalar", (1, 1): "scalar", (2, 0): "scalar", (2, 1): "vector", (3, 0): "vector", (3, 1): "vector"}
+NWORDS = 3
+HEADW = True
+HEADG = 3
+GENG = {2: 0, 3: 0}
+
+
+def tile_resmlpcrosspatchintochannelexpansion_x2_kernel(
+    tc, x, gt, t_words, t_scales, ls, a2, b2, w_words, w_scales, out_0, out_1, out_2
+):
+    nc = tc.nc
+    with ExitStack() as ctx:
+        const = ctx.enter_context(tc.tile_pool(name="const", bufs=1))
+        two = ctx.enter_context(tc.tile_pool(name="two", bufs=2))
+        ypool = ctx.enter_context(tc.tile_pool(name="ypool", bufs=3))
+        opool = ctx.enter_context(tc.tile_pool(name="opool", bufs=6))
+        ppool = ctx.enter_context(tc.tile_pool(name="ppool", bufs=3))
+        qpool = ctx.enter_context(tc.tile_pool(name="qpool", bufs=4))
+        wide = ctx.enter_context(tc.psum_pool(name="wide", bufs=WB))
+        mix = ctx.enter_context(tc.psum_pool(name="mix", bufs=8 - WB))
+        ctx.enter_context(tc.manual_schedule())
+
+        xs = []
+        for b in range(B):
+            xb = const.tile([P, 4, D], BF16, name=f"x{b}", align_bytes=64)
+            xs.append(xb)
+        gtt = const.tile([P, 4], BF16, name="gtt")
+        lst = const.tile([P, 4], BF16, name="lst")
+        a2t = const.tile([P, 4], BF16, name="a2t")
+        b2t = const.tile([P, 4], BF16, name="b2t")
+        a2f = const.tile([P, 4], F32, name="a2f")
+        b2f = const.tile([P, 4], F32, name="b2f")
+        gtf = const.tile([P, 4], F32, name="gtf")
+        la = const.tile([P, 4], F32, name="la")
+        tw = const.tile([P, 2 * S], U8, name="tw", align_bytes=64)
+        ww = const.tile([P, 2 * F], U8, name="ww", align_bytes=64)
+        sc = const.tile([P, S + F], U8, name="sc", align_bytes=64)
+        wp = const.tile([P, 2, 4, P, 2], U8, name="wp", align_bytes=64)
+        wsp = const.tile([P, 2, 4, P], U8, name="wsp", align_bytes=64)
+        ident = const.tile([P, P], F32, name="ident", align_bytes=64)
+        warm = const.tile([P, 1], F32, name="warm")
+        ts = sc[:, 0:S]
+        ws = sc[:, S : S + F]
+
+        def load_x(b, j0, j1):
+            nc.sync.dma_start(
+                out=xs[b][:, j0:j1, :],
+                in_=x[b].rearrange("(p j) d -> p j d", j=4)[:, j0:j1, :],
+            )
+
+        nc.vector.memset(sc[:].bitcast(I32), 0)
+        nc.vector.memset(warm[:], 0.0)
+
+        def load_vec(vec, dst):
+            nc.scalar.dma_start(out=dst[:], in_=vec.rearrange("(p t) -> p t", t=4))
+
+        def load_scales(src, c0, n):
+            for q in range(4):
+                nc.sync.dma_start(
+                    out=sc[32 * q : 32 * q + 4, c0 : c0 + n].bitcast(I32),
+                    in_=src[0, 4 * q : 4 * q + 4, :].bitcast(I32),
+                )
+
+        make_identity(nc, ident[:])
+        load_vec(gt, gtt)
+        load_x(0, 0, 2)
+        load_vec(a2, a2t)
+        load_x(0, 2, 4)
+        load_vec(b2, b2t)
+        nc.sync.dma_start(out=tw[:].bitcast(I32), in_=t_words[0].bitcast(I32))
+        load_vec(ls, lst)
+        load_scales(t_scales, 0, S)
+        load_x(1, 0, 4)
+        nc.sync.dma_start(out=ww[:].bitcast(I32), in_=w_words[0].bitcast(I32))
+        load_scales(w_scales, S, F)
+        load_x(2, 0, 4)
+        load_x(3, 0, 4)
+        nc.scalar.activation(warm[:], warm[:], ACT.Gelu)
+
+        banks = {}
+        ys = {}
+        gs = {}
+        nis = {}
+        nqs = {}
+        ubs = {}
+        uis = {}
+        uqs = {}
+        ps = {}
+        pcs = {}
+        ms = {}
+        gelus = {}
+        obs = {}
+        obanks = {}
+
+        def turn(b, us=(0, 1)):
+            words = xs[b][:].rearrange("p j d -> p (j d)").bitcast(F32)
+            for u in us:
+                bank = mix.tile([P, 4, P], F32, name=f"xt{b}_{u}", tag="m")
+                for j in range(4):
+                    nc.tensor.transpose(
+                        bank[:, j, :], words[:, 256 * j + u : 256 * (j + 1) : 2], ident[:]
+                    )
+                banks[b, u] = bank
+
+        def affine(b, engine, i0=0, n=S, chans=(0, 1, 2, 3)):
+            if b not in ys:
+                y = ypool.tile([P, 4, S], F32, name=f"y{b}", tag="y")
+                ys[b] = y
+            for t in chans:
+                u, e = t // 2, t % 2
+                view = banks[b, u][:].rearrange("p j q -> p (j q)").bitcast(BF16)
+                src = view.rearrange("p (j q e) -> p q j e", j=4, e=2)[:, i0 // 4 : (i0 + n) // 4, :, e]
+                dst = ys[b][:, t, i0 : i0 + n].rearrange("p (q j) -> p q j", j=4)
+                if engine == "scalar":
+                    nc.scalar.activation(
+                        dst, src, ACT.Identity, bias=b2f[:, t : t + 1], scale=a2f[:, t : t + 1]
+                    )
+                else:
+                    nc.vector.tensor_scalar(
+                        dst, src, a2f[:, t : t + 1], b2f[:, t : t + 1], op0=ALU.mult, op1=ALU.add
+                    )
+
+        def gate(b, js, engine="vector"):
+            if b not in gs:
+                g = two.tile([P, 4, D], BF16, name=f"g{b}", tag="g", align_bytes=64)
+                gs[b] = g
+            for j in js:
+                if engine == "scalar":
+                    nc.scalar.activation(
+                        gs[b][:, j, :], xs[b][:, j, :], ACT.Copy, scale=gtf[:, j : j + 1]
+                    )
+                    continue
+                nc.vector.tensor_scalar(
+                    gs[b][:, j, :], xs[b][:, j, :], gtt[:, j : j + 1], None, op0=ALU.mult
+                )
+
+        def weave_n(b, t0=0, t1=4, engine="vector"):
+            if b not in nis:
+                ni = two.tile([P, 4, P, 4], BF16, name=f"ni{b}", tag="ni", align_bytes=64)
+                nis[b] = ni
+            copy = nc.vector.tensor_copy if engine == "vector" else nc.scalar.copy
+            copy(
+                out=nis[b][:, t0:t1], in_=gs[b][:].rearrange("p j (m t) -> p t m j", t=4)[:, t0:t1]
+            )
+
+        def quant_n(b, t0=0, t1=4):
+            if b not in nqs:
+                nq = two.tile([P, D], U32, name=f"nq{b}", tag="nq", align_bytes=64)
+                ns = two.tile([P, D], U8, name=f"ns{b}", tag="ns", align_bytes=64)
+                nqs[b] = (nq, ns)
+            nq, ns = nqs[b]
+            nc.vector.quantize_mx(
+                out=nq[:, P * t0 : P * t1].bitcast(FP8X4),
+                scales=ns[:, P * t0 : P * t1],
+                in_=nis[b][:, t0:t1].rearrange("p t m j -> p (t m j)"),
+            )
+
+        def mix_mm(b, i0, n, groups=None):
+            nq, ns = nqs[b]
+            per = 512 // n
+            for t0 in range(0, 4, per):
+                if groups is not None and t0 // per not in groups:
+                    continue
+                m = mix.tile([P, per, n], F32, name=f"m{b}_{i0}_{t0}", tag="m")
+                for k in range(per):
+                    t = t0 + k
+                    ms[b, i0, t] = m[:, k, :]
+                    nc.tensor.matmul_mx(
+                        out=m[:, k, :],
+                        lhsT=nq[:, P * t : P * (t + 1)].bitcast(FP8X4),
+                        lhsT_scale=ns[:, P * t : P * (t + 1)],
+                        rhs=tw[:, 2 * i0 : 2 * (i0 + n)].bitcast(FP4X4),
+                        rhs_scale=ts[:, i0 : i0 + n],
+                        start=True,
+                        stop=True,
+                    )
+
+        def residual(b, i0, n, chans=(0, 1, 2, 3)):
+            if b not in ubs:
+                ub = two.tile([P, 4, S], BF16, name=f"ub{b}", tag="ub", align_bytes=64)
+                ui = two.tile([P, S, 4], BF16, name=f"ui{b}", tag="ui", align_bytes=64)
+                uq = two.tile([P, S], U32, name=f"uq{b}", tag="uq", align_bytes=64)
+                us = two.tile([P, S], U8, name=f"us{b}", tag="us", align_bytes=64)
+                ubs[b], uis[b], uqs[b] = ub, ui, (uq, us)
+            for t in chans:
+                nc.vector.scalar_tensor_tensor(
+                    ubs[b][:, t, i0 : i0 + n],
+                    ms[b, i0, t],
+                    la[:, t : t + 1],
+                    ys[b][:, t, i0 : i0 + n],
+                    op0=ALU.mult,
+                    op1=ALU.add,
+                )
+
+        def weave_u(b, i0, n):
+            nc.vector.tensor_copy(
+                out=uis[b][:, i0 : i0 + n, :].rearrange("p (c i) t -> p c t i", i=4),
+                in_=ubs[b][:, :, i0 : i0 + n].rearrange("p t (c i) -> p c t i", i=4),
+            )
+
+        def quant_u(b, i0, n):
+            uq, us = uqs[b]
+            nc.vector.quantize_mx(
+                out=uq[:, i0 : i0 + n].bitcast(FP8X4),
+                scales=us[:, i0 : i0 + n],
+                in_=uis[b][:, i0 : i0 + n, :].rearrange("p i t -> p (i t)"),
+            )
+
+        def part_a(b, tb, half=None):
+            uq, us = uqs[b]
+            toks = slice(P * tb, P * (tb + 1))
+            if (b, tb) not in gelus:
+                o = opool.tile([P, F], F32, name=f"o{b}_{tb}", tag="o", align_bytes=64)
+                gelus[b, tb] = o
+            o = gelus[b, tb]
+            for h in range(2) if half is None else (half,):
+                bank = wide.tile([P, 512], F32, name=f"ha{b}_{tb}_{h}", tag="w")
+                nc.tensor.matmul_mx(
+                    out=bank[:],
+                    lhsT=uq[:, toks].bitcast(FP8X4),
+                    lhsT_scale=us[:, toks],
+                    rhs=ww[:, 1024 * h : 1024 * (h + 1)].bitcast(FP4X4),
+                    rhs_scale=ws[:, 512 * h : 512 * (h + 1)],
+                    start=True,
+                    stop=True,
+                )
+                nc.scalar.activation(o[:, 512 * h : 512 * (h + 1)], bank[:], ACT.Gelu)
+            if half != 0:
+                nc.sync.dma_start(out=out_0[b, toks, :], in_=o[:])
+
+        def plane_tile(b):
+            if b not in ps:
+                pt = ppool.tile([P, 2, S, 4], BF16, name=f"p{b}", tag="p", align_bytes=64)
+                ps[b] = pt
+
+        def round_o(b, tb):
+            ob = two.tile([P, F], BF16, name=f"ob{b}_{tb}", tag="ob", align_bytes=64)
+            obs[b, tb] = ob
+            nc.vector.tensor_copy(out=ob[:], in_=gelus[b, tb][:])
+
+        def turn_o(b, tb):
+            words = obs[b, tb][:].bitcast(F32)
+            bank = wide.tile([P, 2, 2, P], F32, name=f"ot{b}_{tb}", tag="w")
+            obanks[b, tb] = bank
+            for g in range(2):
+                for u in range(2):
+                    nc.tensor.transpose(
+                        bank[:, g, u, :], words[:, 256 * g + u : 256 * (g + 1) : 2], ident[:]
+                    )
+
+        def copy_o(b, tb):
+            plane_tile(b)
+            toks = slice(P * tb, P * (tb + 1))
+            for g in range(2):
+                dst = ps[b][:, g, toks, :].rearrange("p r t -> p (r t)").bitcast(F32)
+                nc.vector.tensor_copy(
+                    out=dst.rearrange("p (r u) -> p r u", u=2),
+                    in_=obanks[b, tb][:, g].rearrange("p u r -> p r u"),
+                )
+
+        def part_b(b, g, tb):
+            uq, us = uqs[b]
+            toks = slice(P * tb, P * (tb + 1))
+            plane_tile(b)
+            bank = wide.tile([P, 4, P], F32, name=f"hb{b}_{g}_{tb}", tag="w")
+            for t in range(4):
+                nc.tensor.matmul_mx(
+                    out=bank[:, t, :],
+                    lhsT=wp[:, g, t, :, :].rearrange("p m c -> p (m c)").bitcast(FP4X4),
+                    lhsT_scale=wsp[:, g, t, :],
+                    rhs=uq[:, toks].bitcast(FP8X4),
+                    rhs_scale=us[:, toks],
+                    start=True,
+                    stop=True,
+                )
+            nc.scalar.activation(
+                ps[b][:, g, toks, :], bank[:].rearrange("p t r -> p r t"), ACT.Gelu
+            )
+
+        def planes(b, g, i0, n):
+            if b not in pcs:
+                pc = qpool.tile([P, 2, S], U8, name=f"pc{b}", tag="pc", align_bytes=64)
+                pcs[b] = pc
+            pq = qpool.tile([P, S], U32, name=f"pq{b}_{g}_{i0}", tag="pq", align_bytes=64)
+            nc.vector.quantize_mx(
+                out=pq[:, 0:n].bitcast(FP8X4),
+                scales=pcs[b][:, g, i0 : i0 + n],
+                in_=ps[b][:, g, i0 : i0 + n, :].rearrange("p i t -> p (i t)"),
+            )
+            m0 = b * S + i0
+            nc.sync.dma_start(
+                out=out_1[g, :, m0 : m0 + n, :].rearrange("p m t -> p (m t)").bitcast(I32),
+                in_=pq[:, 0:n].bitcast(I32),
+            )
+
+        def store_scales(b):
+            for q in range(4):
+                nc.sync.dma_start(
+                    out=out_2[:, 4 * q : 4 * q + 4, b * S : (b + 1) * S].rearrange("g q m -> q g m").bitcast(I32),
+                    in_=pcs[b][32 * q : 32 * q + 4, :, :].bitcast(I32),
+                )
+
+        def permute_w(g):
+            nc.vector.tensor_copy(
+                out=wp[:, g],
+                in_=ww[:, 1024 * g : 1024 * (g + 1)].rearrange("p (m t c) -> p t m c", t=4, c=2),
+            )
+
+        def permute_s():
+            nc.vector.tensor_copy(out=wsp[:], in_=ws.rearrange("p (g m t) -> p g t m", g=2, t=4))
+
+        nc.vector.tensor_copy(out=gtf[:], in_=gtt[:])
+        turn(0)
+        gate(0, range(4))
+        weave_n(0, 0, 2)
+        if HEADW:
+            weave_n(0, 3, 4, "scalar")
+        nc.vector.tensor_copy(out=a2f[:], in_=a2t[:])
+        nc.vector.tensor_copy(out=b2f[:], in_=b2t[:])
+        quant_n(0, 0, 2)
+        weave_n(0, 2, 3 if HEADW else 4)
+        nc.vector.tensor_tensor(la[:], lst[:], a2t[:], op=ALU.mult)
+        quant_n(0, 2, 4)
+        affine(0, "scalar", 0, 128)
+        affine(0, "scalar", 128, 384)
+        gate(1, range(HEADG), "scalar")
+        mix_mm(0, 0, 128)
+        mix_mm(0, 128, 128)
+        residual(0, 0, 128)
+        if HEADG < 1:
+            gate(1, (0,))
+        weave_u(0, 0, 128)
+        if HEADG < 2:
+            gate(1, (1,))
+        quant_u(0, 0, 128)
+        part_a(0, 0)
+        residual(0, 128, 128)
+        if HEADG < 3:
+            gate(1, (2,))
+        weave_u(0, 128, 128)
+        if HEADG < 4:
+            gate(1, (3,))
+        quant_u(0, 128, 128)
+        mix_mm(0, 256, 256)
+        part_a(0, 1)
+        residual(0, 256, 256)
+        weave_n(1, 0, 2)
+        weave_u(0, 256, 256)
+        turn(1, (0,))
+        quant_n(1, 0, 2)
+        quant_u(0, 256, 256)
+        affine(1, "scalar", chans=(0, 1))
+        turn(1, (1,))
+        weave_n(1, 2, 4)
+        permute_w(0)
+        quant_n(1, 2, 4)
+        part_a(0, 2)
+        part_a(0, 3)
+        permute_w(1)
+        permute_s()
+        affine(1, "scalar", chans=(2, 3))
+
+        for b in range(1, B):
+            last = b + 1 == B
+            chain = []
+            for u in range(2):
+                if b >= 2:
+                    chain.append([lambda u=u: turn(b, (u,)), lambda u=u: affine(b, YENG[b, u], chans=(2 * u, 2 * u + 1))])
+                for t in (2 * u, 2 * u + 1):
+                    chain.append([lambda t=t: mix_mm(b, 0, 512, (t,)), lambda t=t: residual(b, 0, 512, (t,))])
+            tiles = []
+            if b >= 2:
+                for tb in range(4):
+                    tiles += [lambda tb=tb: part_a(b - 1, tb, 0), lambda tb=tb: part_a(b - 1, tb, 1)]
+            for g in range(2):
+                for tb in range(4):
+                    tiles.append(lambda g=g, tb=tb: part_b(b - 1, g, tb))
+            order = POS[b]
+            for k in range(len(tiles) + 1):
+                for c, pos in enumerate(order):
+                    if pos == k:
+                        for f in chain[c]:
+                            f()
+                if k < len(tiles):
+                    tiles[k]()
+            if not last:
+                gate(b + 1, range(GENG[b + 1]), "scalar")
+                gate(b + 1, range(GENG[b + 1], 4))
+            weave_u(b, 0, 512)
+            if b >= 2:
+                planes(b - 2, 0, 0, 512)
+            elif not last:
+                weave_n(b + 1, 0, 2)
+            quant_u(b, 0, 512)
+            if b >= 2:
+                planes(b - 2, 1, 0, 512)
+                store_scales(b - 2)
+            if not last:
+                weave_n(b + 1, 0 if b >= 2 else 2, 4)
+                quant_n(b + 1)
+
+        b = B - 1
+        part_a(b, 0)
+        planes(b - 1, 0, 0, 512)
+        round_o(b, 0)
+        part_a(b, 1)
+        turn_o(b, 0)
+        planes(b - 1, 1, 0, 512)
+        store_scales(b - 1)
+        round_o(b, 1)
+        copy_o(b, 0)
+        part_a(b, 2)
+        turn_o(b, 1)
+        if NWORDS > 2:
+            round_o(b, 2)
+        copy_o(b, 1)
+        if NWORDS == 2:
+            part_b(b, 0, 2)
+            part_b(b, 1, 2)
+        planes(b, 0, 0, 256)
+        planes(b, 1, 0, 256)
+        part_a(b, 3)
+        if NWORDS > 2:
+            turn_o(b, 2)
+            copy_o(b, 2)
+        if NWORDS > 3:
+            round_o(b, 3)
+            turn_o(b, 3)
+            copy_o(b, 3)
+        else:
+            part_b(b, 0, 3)
+        planes(b, 0, 256, 256)
+        if NWORDS <= 3:
+            part_b(b, 1, 3)
+        planes(b, 1, 256, 256)
+        store_scales(b)

@@ -17,13 +17,14 @@ ACT = mybir.ActivationFunctionType
 ALU = mybir.AluOpType
 
 P = 128
-WB = 4
-POS = {1: [0, 0, 1, 3], 2: [0, 4, 4, 4, 7, 8], 3: [0, 6, 6, 6, 7, 10]}
-YENG = {(1, 0): "scalar", (1, 1): "scalar", (2, 0): "scalar", (2, 1): "vector", (3, 0): "vector", (3, 1): "vector"}
-NWORDS = 3
-HEADW = True
-HEADG = 3
-GENG = {2: 0, 3: 0}
+N_TILES = 16
+MB = 3
+SCALAR_GATES = (0, 2, 4, 4)
+MIX_SLOTS = ((), (0, 0, 1, 1), (2, 3, 3, 4), (6, 6, 7, 7))
+WEAVE_SLOTS = (None, 1, 5, 9)
+AFFINE_SLOTS = (None, 0, 0, 2)
+VECTOR_COPIES = (6, 10)
+PLANE_SLOTS = {8: (0, 0), 10: (0, 1), 12: (1, 0), 13: (1, 1)}
 
 
 def tile_resmlpcrosspatchintochannelexpansion_x2_kernel(
@@ -32,13 +33,13 @@ def tile_resmlpcrosspatchintochannelexpansion_x2_kernel(
     nc = tc.nc
     with ExitStack() as ctx:
         const = ctx.enter_context(tc.tile_pool(name="const", bufs=1))
-        two = ctx.enter_context(tc.tile_pool(name="two", bufs=2))
+        two = ctx.enter_context(tc.tile_pool(name="two", bufs=4))
         ypool = ctx.enter_context(tc.tile_pool(name="ypool", bufs=3))
-        opool = ctx.enter_context(tc.tile_pool(name="opool", bufs=6))
+        opool = ctx.enter_context(tc.tile_pool(name="opool", bufs=7))
         ppool = ctx.enter_context(tc.tile_pool(name="ppool", bufs=3))
-        qpool = ctx.enter_context(tc.tile_pool(name="qpool", bufs=4))
-        wide = ctx.enter_context(tc.psum_pool(name="wide", bufs=WB))
-        mix = ctx.enter_context(tc.psum_pool(name="mix", bufs=8 - WB))
+        qpool = ctx.enter_context(tc.tile_pool(name="qpool", bufs=6))
+        mix = ctx.enter_context(tc.psum_pool(name="mix", bufs=MB))
+        wide = ctx.enter_context(tc.psum_pool(name="wide", bufs=8 - MB))
         ctx.enter_context(tc.manual_schedule())
 
         xs = []
@@ -49,15 +50,13 @@ def tile_resmlpcrosspatchintochannelexpansion_x2_kernel(
         lst = const.tile([P, 4], BF16, name="lst")
         a2t = const.tile([P, 4], BF16, name="a2t")
         b2t = const.tile([P, 4], BF16, name="b2t")
+        gtf = const.tile([P, 4], F32, name="gtf")
         a2f = const.tile([P, 4], F32, name="a2f")
         b2f = const.tile([P, 4], F32, name="b2f")
-        gtf = const.tile([P, 4], F32, name="gtf")
         la = const.tile([P, 4], F32, name="la")
         tw = const.tile([P, 2 * S], U8, name="tw", align_bytes=64)
         ww = const.tile([P, 2 * F], U8, name="ww", align_bytes=64)
         sc = const.tile([P, S + F], U8, name="sc", align_bytes=64)
-        wp = const.tile([P, 2, 4, P, 2], U8, name="wp", align_bytes=64)
-        wsp = const.tile([P, 2, 4, P], U8, name="wsp", align_bytes=64)
         ident = const.tile([P, P], F32, name="ident", align_bytes=64)
         warm = const.tile([P, 1], F32, name="warm")
         ts = sc[:, 0:S]
@@ -69,11 +68,8 @@ def tile_resmlpcrosspatchintochannelexpansion_x2_kernel(
                 in_=x[b].rearrange("(p j) d -> p j d", j=4)[:, j0:j1, :],
             )
 
-        nc.vector.memset(sc[:].bitcast(I32), 0)
-        nc.vector.memset(warm[:], 0.0)
-
-        def load_vec(vec, dst):
-            nc.scalar.dma_start(out=dst[:], in_=vec.rearrange("(p t) -> p t", t=4))
+        def load_vec(vec, dst, engine):
+            engine.dma_start(out=dst[:], in_=vec.rearrange("(p t) -> p t", t=4))
 
         def load_scales(src, c0, n):
             for q in range(4):
@@ -82,14 +78,16 @@ def tile_resmlpcrosspatchintochannelexpansion_x2_kernel(
                     in_=src[0, 4 * q : 4 * q + 4, :].bitcast(I32),
                 )
 
+        nc.vector.memset(sc[:].bitcast(I32), 0)
+        nc.vector.memset(warm[:], 0.0)
         make_identity(nc, ident[:])
-        load_vec(gt, gtt)
+        load_vec(gt, gtt, nc.scalar)
         load_x(0, 0, 2)
-        load_vec(a2, a2t)
         load_x(0, 2, 4)
-        load_vec(b2, b2t)
-        nc.sync.dma_start(out=tw[:].bitcast(I32), in_=t_words[0].bitcast(I32))
-        load_vec(ls, lst)
+        load_vec(a2, a2t, nc.scalar)
+        load_vec(b2, b2t, nc.scalar)
+        nc.gpsimd.dma_start(out=tw[:].bitcast(I32), in_=t_words[0].bitcast(I32))
+        load_vec(ls, lst, nc.gpsimd)
         load_scales(t_scales, 0, S)
         load_x(1, 0, 4)
         nc.sync.dma_start(out=ww[:].bitcast(I32), in_=w_words[0].bitcast(I32))
@@ -97,361 +95,276 @@ def tile_resmlpcrosspatchintochannelexpansion_x2_kernel(
         load_x(2, 0, 4)
         load_x(3, 0, 4)
         nc.scalar.activation(warm[:], warm[:], ACT.Gelu)
+        nc.vector.tensor_copy(out=gtf[:], in_=gtt[:])
+        nc.vector.tensor_copy(out=a2f[:], in_=a2t[:])
+        nc.vector.tensor_copy(out=b2f[:], in_=b2t[:])
 
-        banks = {}
-        ys = {}
-        gs = {}
-        nis = {}
-        nqs = {}
-        ubs = {}
-        uis = {}
-        uqs = {}
-        ps = {}
-        pcs = {}
-        ms = {}
-        gelus = {}
-        obs = {}
-        obanks = {}
+        live = {}
 
-        def turn(b, us=(0, 1)):
-            words = xs[b][:].rearrange("p j d -> p (j d)").bitcast(F32)
-            for u in us:
-                bank = mix.tile([P, 4, P], F32, name=f"xt{b}_{u}", tag="m")
-                for j in range(4):
-                    nc.tensor.transpose(
-                        bank[:, j, :], words[:, 256 * j + u : 256 * (j + 1) : 2], ident[:]
-                    )
-                banks[b, u] = bank
+        def get(pool, shape, dtype, kind, b):
+            if (kind, b) not in live:
+                live[kind, b] = pool.tile(
+                    shape, dtype, name=f"{kind}_{b}", tag=kind, align_bytes=64
+                )
+            return live[kind, b]
 
-        def affine(b, engine, i0=0, n=S, chans=(0, 1, 2, 3)):
-            if b not in ys:
-                y = ypool.tile([P, 4, S], F32, name=f"y{b}", tag="y")
-                ys[b] = y
-            for t in chans:
-                u, e = t // 2, t % 2
-                view = banks[b, u][:].rearrange("p j q -> p (j q)").bitcast(BF16)
-                src = view.rearrange("p (j q e) -> p q j e", j=4, e=2)[:, i0 // 4 : (i0 + n) // 4, :, e]
-                dst = ys[b][:, t, i0 : i0 + n].rearrange("p (q j) -> p q j", j=4)
-                if engine == "scalar":
-                    nc.scalar.activation(
-                        dst, src, ACT.Identity, bias=b2f[:, t : t + 1], scale=a2f[:, t : t + 1]
-                    )
-                else:
+        def gate(b, engine):
+            g = get(two, [P, 4, D], BF16, "gated", b)
+            for j in range(4):
+                if j < SCALAR_GATES[b]:
+                    if engine == "scalar":
+                        nc.scalar.activation(
+                            g[:, j, :], xs[b][:, j, :], ACT.Copy, scale=gtf[:, j : j + 1]
+                        )
+                elif engine == "vector":
                     nc.vector.tensor_scalar(
-                        dst, src, a2f[:, t : t + 1], b2f[:, t : t + 1], op0=ALU.mult, op1=ALU.add
-                    )
-
-        def gate(b, js, engine="vector"):
-            if b not in gs:
-                g = two.tile([P, 4, D], BF16, name=f"g{b}", tag="g", align_bytes=64)
-                gs[b] = g
-            for j in js:
-                if engine == "scalar":
-                    nc.scalar.activation(
-                        gs[b][:, j, :], xs[b][:, j, :], ACT.Copy, scale=gtf[:, j : j + 1]
-                    )
-                    continue
-                nc.vector.tensor_scalar(
-                    gs[b][:, j, :], xs[b][:, j, :], gtt[:, j : j + 1], None, op0=ALU.mult
+                    g[:, j, :], xs[b][:, j, :], gtt[:, j : j + 1], None, op0=ALU.mult
                 )
 
-        def weave_n(b, t0=0, t1=4, engine="vector"):
-            if b not in nis:
-                ni = two.tile([P, 4, P, 4], BF16, name=f"ni{b}", tag="ni", align_bytes=64)
-                nis[b] = ni
+        def weave_n(b, m0, m1, engine):
+            g = get(two, [P, 4, D], BF16, "gated", b)
+            ni = get(two, [P, 4, P, 4], BF16, "nwoven", b)
             copy = nc.vector.tensor_copy if engine == "vector" else nc.scalar.copy
             copy(
-                out=nis[b][:, t0:t1], in_=gs[b][:].rearrange("p j (m t) -> p t m j", t=4)[:, t0:t1]
+                out=ni[:, :, m0:m1, :].rearrange("p t m j -> p m j t"),
+                in_=g[:].rearrange("p j (m t) -> p m j t", t=4)[:, m0:m1],
             )
 
-        def quant_n(b, t0=0, t1=4):
-            if b not in nqs:
-                nq = two.tile([P, D], U32, name=f"nq{b}", tag="nq", align_bytes=64)
-                ns = two.tile([P, D], U8, name=f"ns{b}", tag="ns", align_bytes=64)
-                nqs[b] = (nq, ns)
-            nq, ns = nqs[b]
+        def quant_n(b, t0, t1):
+            ni = get(two, [P, 4, P, 4], BF16, "nwoven", b)
+            nq = get(two, [P, D], U32, "ncodes", b)
+            ns = get(two, [P, D], U8, "nscales", b)
             nc.vector.quantize_mx(
                 out=nq[:, P * t0 : P * t1].bitcast(FP8X4),
                 scales=ns[:, P * t0 : P * t1],
-                in_=nis[b][:, t0:t1].rearrange("p t m j -> p (t m j)"),
+                in_=ni[:, t0:t1].rearrange("p t m j -> p (t m j)"),
             )
 
-        def mix_mm(b, i0, n, groups=None):
-            nq, ns = nqs[b]
-            per = 512 // n
-            for t0 in range(0, 4, per):
-                if groups is not None and t0 // per not in groups:
-                    continue
-                m = mix.tile([P, per, n], F32, name=f"m{b}_{i0}_{t0}", tag="m")
-                for k in range(per):
-                    t = t0 + k
-                    ms[b, i0, t] = m[:, k, :]
-                    nc.tensor.matmul_mx(
-                        out=m[:, k, :],
-                        lhsT=nq[:, P * t : P * (t + 1)].bitcast(FP8X4),
-                        lhsT_scale=ns[:, P * t : P * (t + 1)],
-                        rhs=tw[:, 2 * i0 : 2 * (i0 + n)].bitcast(FP4X4),
-                        rhs_scale=ts[:, i0 : i0 + n],
-                        start=True,
-                        stop=True,
-                    )
+        def turn_x(b, u, pool, tag):
+            words = xs[b][:].rearrange("p j d -> p (j d)").bitcast(F32)
+            bank = pool.tile([P, 4, P], F32, name=f"xt{b}_{u}", tag=tag)
+            live["xt", b, u] = bank
+            for j in range(4):
+                nc.tensor.transpose(
+                    bank[:, j, :], words[:, 256 * j + u : 256 * (j + 1) : 2], ident[:]
+                )
 
-        def residual(b, i0, n, chans=(0, 1, 2, 3)):
-            if b not in ubs:
-                ub = two.tile([P, 4, S], BF16, name=f"ub{b}", tag="ub", align_bytes=64)
-                ui = two.tile([P, S, 4], BF16, name=f"ui{b}", tag="ui", align_bytes=64)
-                uq = two.tile([P, S], U32, name=f"uq{b}", tag="uq", align_bytes=64)
-                us = two.tile([P, S], U8, name=f"us{b}", tag="us", align_bytes=64)
-                ubs[b], uis[b], uqs[b] = ub, ui, (uq, us)
+        def affine(b, u, i0=0, n=S):
+            y = get(ypool, [P, 4, S], F32, "y", b)
+            view = live["xt", b, u][:].rearrange("p j q -> p (j q)").bitcast(BF16)
+            view = view.rearrange("p (j q e) -> p q j e", j=4, e=2)
+            for e in range(2):
+                t = 2 * u + e
+                nc.scalar.activation(
+                    y[:, t, i0 : i0 + n].rearrange("p (q j) -> p q j", j=4),
+                    view[:, i0 // 4 : (i0 + n) // 4, :, e],
+                    ACT.Identity,
+                    bias=b2f[:, t : t + 1],
+                    scale=a2f[:, t : t + 1],
+                )
+
+        def mix_mm(b, i0, n, chans):
+            nq = get(two, [P, D], U32, "ncodes", b)
+            ns = get(two, [P, D], U8, "nscales", b)
+            per = 512 // n
+            for t in chans:
+                if t % per == 0:
+                    bank = mix.tile([P, per, n], F32, name=f"m{b}_{i0}_{t}", tag="m")
+                live["m", b, i0, t] = bank[:, t % per, :]
+                cols = slice(P * t, P * (t + 1))
+                nc.tensor.matmul_mx(
+                    out=bank[:, t % per, :],
+                    lhsT=nq[:, cols].bitcast(FP8X4),
+                    lhsT_scale=ns[:, cols],
+                    rhs=tw[:, 2 * i0 : 2 * (i0 + n)].bitcast(FP4X4),
+                    rhs_scale=ts[:, i0 : i0 + n],
+                    start=True,
+                    stop=True,
+                )
+
+        def residual(b, i0, n, chans=range(4)):
+            y = get(ypool, [P, 4, S], F32, "y", b)
+            ub = get(two, [P, 4, S], BF16, "u", b)
             for t in chans:
                 nc.vector.scalar_tensor_tensor(
-                    ubs[b][:, t, i0 : i0 + n],
-                    ms[b, i0, t],
+                    ub[:, t, i0 : i0 + n],
+                    live["m", b, i0, t],
                     la[:, t : t + 1],
-                    ys[b][:, t, i0 : i0 + n],
+                    y[:, t, i0 : i0 + n],
                     op0=ALU.mult,
                     op1=ALU.add,
                 )
 
         def weave_u(b, i0, n):
+            ub = get(two, [P, 4, S], BF16, "u", b)
+            ui = get(two, [P, S, 4], BF16, "uwoven", b)
             nc.vector.tensor_copy(
-                out=uis[b][:, i0 : i0 + n, :].rearrange("p (c i) t -> p c t i", i=4),
-                in_=ubs[b][:, :, i0 : i0 + n].rearrange("p t (c i) -> p c t i", i=4),
+                out=ui[:, i0 : i0 + n, :].rearrange("p (c i) t -> p c t i", i=4),
+                in_=ub[:, :, i0 : i0 + n].rearrange("p t (c i) -> p c t i", i=4),
             )
 
         def quant_u(b, i0, n):
-            uq, us = uqs[b]
+            ui = get(two, [P, S, 4], BF16, "uwoven", b)
+            uq = get(two, [P, S], U32, "ucodes", b)
+            us = get(two, [P, S], U8, "uscales", b)
             nc.vector.quantize_mx(
                 out=uq[:, i0 : i0 + n].bitcast(FP8X4),
                 scales=us[:, i0 : i0 + n],
-                in_=uis[b][:, i0 : i0 + n, :].rearrange("p i t -> p (i t)"),
+                in_=ui[:, i0 : i0 + n, :].rearrange("p i t -> p (i t)"),
             )
 
-        def part_a(b, tb, half=None):
-            uq, us = uqs[b]
+        def project(k):
+            b, tb = divmod(k, 4)
+            uq = get(two, [P, S], U32, "ucodes", b)
+            us = get(two, [P, S], U8, "uscales", b)
+            o = get(opool, [P, F], F32, "o", k)
             toks = slice(P * tb, P * (tb + 1))
-            if (b, tb) not in gelus:
-                o = opool.tile([P, F], F32, name=f"o{b}_{tb}", tag="o", align_bytes=64)
-                gelus[b, tb] = o
-            o = gelus[b, tb]
-            for h in range(2) if half is None else (half,):
-                bank = wide.tile([P, 512], F32, name=f"ha{b}_{tb}_{h}", tag="w")
+            for h in range(2):
+                cols = slice(512 * h, 512 * (h + 1))
+                bank = wide.tile([P, 512], F32, name=f"h{k}_{h}", tag="w")
                 nc.tensor.matmul_mx(
                     out=bank[:],
                     lhsT=uq[:, toks].bitcast(FP8X4),
                     lhsT_scale=us[:, toks],
                     rhs=ww[:, 1024 * h : 1024 * (h + 1)].bitcast(FP4X4),
-                    rhs_scale=ws[:, 512 * h : 512 * (h + 1)],
+                    rhs_scale=ws[:, cols],
                     start=True,
                     stop=True,
                 )
-                nc.scalar.activation(o[:, 512 * h : 512 * (h + 1)], bank[:], ACT.Gelu)
-            if half != 0:
-                nc.sync.dma_start(out=out_0[b, toks, :], in_=o[:])
+                nc.scalar.activation(o[:, cols], bank[:], ACT.Gelu)
+            nc.sync.dma_start(out=out_0[b, toks, :], in_=o[:])
 
-        def plane_tile(b):
-            if b not in ps:
-                pt = ppool.tile([P, 2, S, 4], BF16, name=f"p{b}", tag="p", align_bytes=64)
-                ps[b] = pt
+        def round_o(k):
+            ob = get(qpool, [P, F], BF16, "orounded", k)
+            nc.vector.tensor_copy(out=ob[:], in_=live["o", k][:])
 
-        def round_o(b, tb):
-            ob = two.tile([P, F], BF16, name=f"ob{b}_{tb}", tag="ob", align_bytes=64)
-            obs[b, tb] = ob
-            nc.vector.tensor_copy(out=ob[:], in_=gelus[b, tb][:])
-
-        def turn_o(b, tb):
-            words = obs[b, tb][:].bitcast(F32)
-            bank = wide.tile([P, 2, 2, P], F32, name=f"ot{b}_{tb}", tag="w")
-            obanks[b, tb] = bank
+        def turn_o(k):
+            words = live["orounded", k][:].bitcast(F32)
+            bank = wide.tile([P, 2, 2, P], F32, name=f"ot{k}", tag="w")
+            live["ot", k] = bank
             for g in range(2):
                 for u in range(2):
                     nc.tensor.transpose(
                         bank[:, g, u, :], words[:, 256 * g + u : 256 * (g + 1) : 2], ident[:]
                     )
 
-        def copy_o(b, tb):
-            plane_tile(b)
-            toks = slice(P * tb, P * (tb + 1))
+        def copy_o(k):
+            b, tb = divmod(k, 4)
+            pt = get(ppool, [P, 2, S, 4], BF16, "pwoven", b)
+            copy = nc.vector.tensor_copy if k in VECTOR_COPIES else nc.scalar.copy
             for g in range(2):
-                dst = ps[b][:, g, toks, :].rearrange("p r t -> p (r t)").bitcast(F32)
-                nc.vector.tensor_copy(
-                    out=dst.rearrange("p (r u) -> p r u", u=2),
-                    in_=obanks[b, tb][:, g].rearrange("p u r -> p r u"),
+                dst = pt[:, g, P * tb : P * (tb + 1), :].rearrange("p r t -> p (r t)")
+                copy(
+                    out=dst.bitcast(F32).rearrange("p (r u) -> p r u", u=2),
+                    in_=live["ot", k][:, g].rearrange("p u r -> p r u"),
                 )
-
-        def part_b(b, g, tb):
-            uq, us = uqs[b]
-            toks = slice(P * tb, P * (tb + 1))
-            plane_tile(b)
-            bank = wide.tile([P, 4, P], F32, name=f"hb{b}_{g}_{tb}", tag="w")
-            for t in range(4):
-                nc.tensor.matmul_mx(
-                    out=bank[:, t, :],
-                    lhsT=wp[:, g, t, :, :].rearrange("p m c -> p (m c)").bitcast(FP4X4),
-                    lhsT_scale=wsp[:, g, t, :],
-                    rhs=uq[:, toks].bitcast(FP8X4),
-                    rhs_scale=us[:, toks],
-                    start=True,
-                    stop=True,
-                )
-            nc.scalar.activation(
-                ps[b][:, g, toks, :], bank[:].rearrange("p t r -> p r t"), ACT.Gelu
-            )
 
         def planes(b, g, i0, n):
-            if b not in pcs:
-                pc = qpool.tile([P, 2, S], U8, name=f"pc{b}", tag="pc", align_bytes=64)
-                pcs[b] = pc
-            pq = qpool.tile([P, S], U32, name=f"pq{b}_{g}_{i0}", tag="pq", align_bytes=64)
+            pt = live["pwoven", b]
+            pc = get(two, [P, 2, 2 * S], U8, "pscales", b // 2)
+            pq = get(qpool, [P, S], U32, "pcodes", (b, g, i0))
+            c0 = b % 2 * S + i0
+            m0 = b * S + i0
             nc.vector.quantize_mx(
                 out=pq[:, 0:n].bitcast(FP8X4),
-                scales=pcs[b][:, g, i0 : i0 + n],
-                in_=ps[b][:, g, i0 : i0 + n, :].rearrange("p i t -> p (i t)"),
+                scales=pc[:, g, c0 : c0 + n],
+                in_=pt[:, g, i0 : i0 + n, :].rearrange("p i t -> p (i t)"),
             )
-            m0 = b * S + i0
             nc.sync.dma_start(
                 out=out_1[g, :, m0 : m0 + n, :].rearrange("p m t -> p (m t)").bitcast(I32),
                 in_=pq[:, 0:n].bitcast(I32),
             )
 
-        def store_scales(b):
+        def store_scales(pair):
+            m0 = 2 * S * pair
             for q in range(4):
                 nc.sync.dma_start(
-                    out=out_2[:, 4 * q : 4 * q + 4, b * S : (b + 1) * S].rearrange("g q m -> q g m").bitcast(I32),
-                    in_=pcs[b][32 * q : 32 * q + 4, :, :].bitcast(I32),
+                    out=out_2[:, 4 * q : 4 * q + 4, m0 : m0 + 2 * S]
+                    .rearrange("g q m -> q g m")
+                    .bitcast(I32),
+                    in_=live["pscales", pair][32 * q : 32 * q + 4, :, :].bitcast(I32),
                 )
 
-        def permute_w(g):
-            nc.vector.tensor_copy(
-                out=wp[:, g],
-                in_=ww[:, 1024 * g : 1024 * (g + 1)].rearrange("p (m t c) -> p t m c", t=4, c=2),
-            )
-
-        def permute_s():
-            nc.vector.tensor_copy(out=wsp[:], in_=ws.rearrange("p (g m t) -> p g t m", g=2, t=4))
-
-        nc.vector.tensor_copy(out=gtf[:], in_=gtt[:])
-        turn(0)
-        gate(0, range(4))
-        weave_n(0, 0, 2)
-        if HEADW:
-            weave_n(0, 3, 4, "scalar")
-        nc.vector.tensor_copy(out=a2f[:], in_=a2t[:])
-        nc.vector.tensor_copy(out=b2f[:], in_=b2t[:])
+        turn_x(0, 0, wide, "w")
+        turn_x(0, 1, wide, "w")
+        gate(0, "vector")
+        weave_n(0, 0, 96, "vector")
+        weave_n(0, 96, 128, "scalar")
         quant_n(0, 0, 2)
-        weave_n(0, 2, 3 if HEADW else 4)
-        nc.vector.tensor_tensor(la[:], lst[:], a2t[:], op=ALU.mult)
         quant_n(0, 2, 4)
-        affine(0, "scalar", 0, 128)
-        affine(0, "scalar", 128, 384)
-        gate(1, range(HEADG), "scalar")
-        mix_mm(0, 0, 128)
-        mix_mm(0, 128, 128)
-        residual(0, 0, 128)
-        if HEADG < 1:
-            gate(1, (0,))
-        weave_u(0, 0, 128)
-        if HEADG < 2:
-            gate(1, (1,))
-        quant_u(0, 0, 128)
-        part_a(0, 0)
-        residual(0, 128, 128)
-        if HEADG < 3:
-            gate(1, (2,))
-        weave_u(0, 128, 128)
-        if HEADG < 4:
-            gate(1, (3,))
-        quant_u(0, 128, 128)
-        mix_mm(0, 256, 256)
-        part_a(0, 1)
-        residual(0, 256, 256)
-        weave_n(1, 0, 2)
-        weave_u(0, 256, 256)
-        turn(1, (0,))
-        quant_n(1, 0, 2)
-        quant_u(0, 256, 256)
-        affine(1, "scalar", chans=(0, 1))
-        turn(1, (1,))
-        weave_n(1, 2, 4)
-        permute_w(0)
-        quant_n(1, 2, 4)
-        part_a(0, 2)
-        part_a(0, 3)
-        permute_w(1)
-        permute_s()
-        affine(1, "scalar", chans=(2, 3))
-
-        for b in range(1, B):
-            last = b + 1 == B
-            chain = []
+        nc.vector.tensor_tensor(la[:], lst[:], a2t[:], op=ALU.mult)
+        for i0, n in ((0, 128), (128, 384)):
             for u in range(2):
-                if b >= 2:
-                    chain.append([lambda u=u: turn(b, (u,)), lambda u=u: affine(b, YENG[b, u], chans=(2 * u, 2 * u + 1))])
-                for t in (2 * u, 2 * u + 1):
-                    chain.append([lambda t=t: mix_mm(b, 0, 512, (t,)), lambda t=t: residual(b, 0, 512, (t,))])
-            tiles = []
-            if b >= 2:
-                for tb in range(4):
-                    tiles += [lambda tb=tb: part_a(b - 1, tb, 0), lambda tb=tb: part_a(b - 1, tb, 1)]
-            for g in range(2):
-                for tb in range(4):
-                    tiles.append(lambda g=g, tb=tb: part_b(b - 1, g, tb))
-            order = POS[b]
-            for k in range(len(tiles) + 1):
-                for c, pos in enumerate(order):
-                    if pos == k:
-                        for f in chain[c]:
-                            f()
-                if k < len(tiles):
-                    tiles[k]()
-            if not last:
-                gate(b + 1, range(GENG[b + 1]), "scalar")
-                gate(b + 1, range(GENG[b + 1], 4))
-            weave_u(b, 0, 512)
-            if b >= 2:
-                planes(b - 2, 0, 0, 512)
-            elif not last:
-                weave_n(b + 1, 0, 2)
-            quant_u(b, 0, 512)
-            if b >= 2:
-                planes(b - 2, 1, 0, 512)
-                store_scales(b - 2)
-            if not last:
-                weave_n(b + 1, 0 if b >= 2 else 2, 4)
-                quant_n(b + 1)
+                affine(0, u, i0, n)
+        gate(1, "scalar")
+        mix_mm(0, 0, 128, range(4))
+        mix_mm(0, 128, 128, range(4))
+        residual(0, 0, 128)
+        gate(1, "vector")
+        weave_u(0, 0, 128)
+        residual(0, 128, 128)
+        quant_u(0, 0, 128)
+        mix_mm(0, 256, 256, range(4))
+        weave_u(0, 128, 128)
+        residual(0, 256, 256, (0, 1))
+        quant_u(0, 128, 128)
+        residual(0, 256, 256, (2, 3))
+        weave_u(0, 256, 256)
+        weave_n(1, 0, 128, "vector")
+        quant_u(0, 256, 256)
+        quant_n(1, 0, 2)
+        quant_n(1, 2, 4)
 
-        b = B - 1
-        part_a(b, 0)
-        planes(b - 1, 0, 0, 512)
-        round_o(b, 0)
-        part_a(b, 1)
-        turn_o(b, 0)
-        planes(b - 1, 1, 0, 512)
-        store_scales(b - 1)
-        round_o(b, 1)
-        copy_o(b, 0)
-        part_a(b, 2)
-        turn_o(b, 1)
-        if NWORDS > 2:
-            round_o(b, 2)
-        copy_o(b, 1)
-        if NWORDS == 2:
-            part_b(b, 0, 2)
-            part_b(b, 1, 2)
-        planes(b, 0, 0, 256)
-        planes(b, 1, 0, 256)
-        part_a(b, 3)
-        if NWORDS > 2:
-            turn_o(b, 2)
-            copy_o(b, 2)
-        if NWORDS > 3:
-            round_o(b, 3)
-            turn_o(b, 3)
-            copy_o(b, 3)
-        else:
-            part_b(b, 0, 3)
-        planes(b, 0, 256, 256)
-        if NWORDS <= 3:
-            part_b(b, 1, 3)
-        planes(b, 1, 256, 256)
-        store_scales(b)
+        for k in range(N_TILES):
+            if k >= 2:
+                round_o(k - 2)
+            if k == 0:
+                for c in (2, 3):
+                    gate(c, "scalar")
+                for c in (2, 3):
+                    weave_n(c, 0, 128, "vector")
+            for c in range(1, B):
+                if AFFINE_SLOTS[c] == k:
+                    for u in range(2):
+                        turn_x(c, u, mix, "m")
+                        affine(c, u)
+            project(k)
+            if k >= 4:
+                turn_o(k - 4)
+            for c in range(1, B):
+                if WEAVE_SLOTS[c] == k - 1:
+                    quant_u(c, 0, 512)
+            if k >= 4:
+                copy_o(k - 4)
+            if k in PLANE_SLOTS:
+                planes(*PLANE_SLOTS[k], 0, 512)
+                if PLANE_SLOTS[k] == (1, 1):
+                    store_scales(0)
+            for c in range(1, B):
+                chans = [t for t in range(4) if MIX_SLOTS[c][t] == k]
+                mix_mm(c, 0, 512, chans)
+                residual(c, 0, 512, chans)
+            if k < 2:
+                quant_n(k + 2, 0, 2)
+                quant_n(k + 2, 2, 4)
+            for c in range(1, B):
+                if WEAVE_SLOTS[c] == k:
+                    weave_u(c, 0, 512)
+
+        round_o(14)
+        turn_o(12)
+        turn_o(13)
+        copy_o(12)
+        round_o(15)
+        turn_o(14)
+        copy_o(13)
+        turn_o(15)
+        for g in range(2):
+            planes(3, g, 0, 256)
+        copy_o(14)
+        copy_o(15)
+        for g in range(2):
+            planes(2, g, 0, 512)
+        for g in range(2):
+            planes(3, g, 256, 256)
+        store_scales(1)

@@ -17,14 +17,24 @@ ACT = mybir.ActivationFunctionType
 ALU = mybir.AluOpType
 
 P = 128
-N_TILES = 16
-MB = 3
-SCALAR_GATES = (0, 2, 4, 4)
-MIX_SLOTS = ((), (0, 0, 1, 1), (2, 3, 3, 4), (6, 6, 7, 7))
-WEAVE_SLOTS = (None, 1, 5, 9)
-AFFINE_SLOTS = (None, 0, 0, 2)
-VECTOR_COPIES = (6, 10)
-PLANE_SLOTS = {8: (0, 0), 10: (0, 1), 12: (1, 0), 13: (1, 1)}
+BANK = 512
+N_TILES = B * S // P
+
+STEPS = {
+    1: dict(affine=(0, 0), mix=(0, 1, 1, 1), weave_u=3, quant_u=4),
+    2: dict(gate_scalar=0, weave_n=0, quant_n=1, affine=(0, 0), mix=(2, 3, 4, 4), weave_u=7, quant_u=7),
+    3: dict(
+        gate_scalar=1, gate_vector=0, weave_n=6, quant_n=7, affine=(4, 7), mix=(8, 8, 9, 9), weave_u=11, quant_u=11
+    ),
+}
+SCALAR_GATES = (0, 2, 4, 3)
+VECTOR_WEAVE = 96
+VECTOR_COPIES = (4, 9, 12)
+PLANE_SLOTS = {12: ((0, 0),), 13: ((0, 1),), 14: ((1, 0), (1, 1))}
+
+
+def round_slot(k):
+    return max(k + 3, 8 + 5 * k // 8)
 
 
 def tile_resmlpcrosspatchintochannelexpansion_x2_kernel(
@@ -33,34 +43,33 @@ def tile_resmlpcrosspatchintochannelexpansion_x2_kernel(
     nc = tc.nc
     with ExitStack() as ctx:
         const = ctx.enter_context(tc.tile_pool(name="const", bufs=1))
-        two = ctx.enter_context(tc.tile_pool(name="two", bufs=4))
-        ypool = ctx.enter_context(tc.tile_pool(name="ypool", bufs=3))
-        opool = ctx.enter_context(tc.tile_pool(name="opool", bufs=7))
-        ppool = ctx.enter_context(tc.tile_pool(name="ppool", bufs=3))
-        qpool = ctx.enter_context(tc.tile_pool(name="qpool", bufs=6))
-        mix = ctx.enter_context(tc.psum_pool(name="mix", bufs=MB))
-        wide = ctx.enter_context(tc.psum_pool(name="wide", bufs=8 - MB))
+        pair = ctx.enter_context(tc.tile_pool(name="pair", bufs=2))
+        three = ctx.enter_context(tc.tile_pool(name="three", bufs=3))
+        results = ctx.enter_context(tc.tile_pool(name="results", bufs=12))
+        rounded_pool = ctx.enter_context(tc.tile_pool(name="rounded", bufs=4))
+        codes_pool = ctx.enter_context(tc.tile_pool(name="codes", bufs=6))
+        mix_banks = ctx.enter_context(tc.psum_pool(name="mix_banks", bufs=3))
+        wide_banks = ctx.enter_context(tc.psum_pool(name="wide_banks", bufs=5))
         ctx.enter_context(tc.manual_schedule())
 
         xs = []
         for b in range(B):
             xb = const.tile([P, 4, D], BF16, name=f"x{b}", align_bytes=64)
             xs.append(xb)
-        gtt = const.tile([P, 4], BF16, name="gtt")
-        lst = const.tile([P, 4], BF16, name="lst")
-        a2t = const.tile([P, 4], BF16, name="a2t")
-        b2t = const.tile([P, 4], BF16, name="b2t")
-        gtf = const.tile([P, 4], F32, name="gtf")
-        a2f = const.tile([P, 4], F32, name="a2f")
-        b2f = const.tile([P, 4], F32, name="b2f")
-        la = const.tile([P, 4], F32, name="la")
-        tw = const.tile([P, 2 * S], U8, name="tw", align_bytes=64)
-        ww = const.tile([P, 2 * F], U8, name="ww", align_bytes=64)
-        sc = const.tile([P, S + F], U8, name="sc", align_bytes=64)
+        gt_bf = const.tile([P, 4], BF16, name="gt_bf")
+        ls_bf = const.tile([P, 4], BF16, name="ls_bf")
+        a2_bf = const.tile([P, 4], BF16, name="a2_bf")
+        b2_bf = const.tile([P, 4], BF16, name="b2_bf")
+        a2_f32 = const.tile([P, 4], F32, name="a2_f32")
+        b2_f32 = const.tile([P, 4], F32, name="b2_f32")
+        ls_a2 = const.tile([P, 4], F32, name="ls_a2")
+        gt_f32 = const.tile([P, 4], F32, name="gt_f32")
+        t_codes = const.tile([P, 2 * S], U8, name="t_codes", align_bytes=64)
+        w_codes = const.tile([P, 2 * F], U8, name="w_codes", align_bytes=64)
+        scales = const.tile([P, S + F], U8, name="scales", align_bytes=64)
         ident = const.tile([P, P], F32, name="ident", align_bytes=64)
-        warm = const.tile([P, 1], F32, name="warm")
-        ts = sc[:, 0:S]
-        ws = sc[:, S : S + F]
+        t_sc = scales[:, 0:S]
+        w_sc = scales[:, S : S + F]
 
         def load_x(b, j0, j1):
             nc.sync.dma_start(
@@ -68,303 +77,287 @@ def tile_resmlpcrosspatchintochannelexpansion_x2_kernel(
                 in_=x[b].rearrange("(p j) d -> p j d", j=4)[:, j0:j1, :],
             )
 
-        def load_vec(vec, dst, engine):
-            engine.dma_start(out=dst[:], in_=vec.rearrange("(p t) -> p t", t=4))
+        def load_vector(engine, dst, src):
+            engine.dma_start(out=dst[:], in_=src.rearrange("(p t) -> p t", t=4))
 
-        def load_scales(src, c0, n):
+        def load_scales(dst, src):
             for q in range(4):
                 nc.sync.dma_start(
-                    out=sc[32 * q : 32 * q + 4, c0 : c0 + n].bitcast(I32),
+                    out=dst[32 * q : 32 * q + 4, :].bitcast(I32),
                     in_=src[0, 4 * q : 4 * q + 4, :].bitcast(I32),
                 )
 
-        nc.vector.memset(sc[:].bitcast(I32), 0)
-        nc.vector.memset(warm[:], 0.0)
+        nc.vector.memset(scales[:].bitcast(I32), 0)
         make_identity(nc, ident[:])
-        load_vec(gt, gtt, nc.scalar)
+        load_vector(nc.scalar, gt_bf, gt)
         load_x(0, 0, 2)
         load_x(0, 2, 4)
-        load_vec(a2, a2t, nc.scalar)
-        load_vec(b2, b2t, nc.scalar)
-        nc.gpsimd.dma_start(out=tw[:].bitcast(I32), in_=t_words[0].bitcast(I32))
-        load_vec(ls, lst, nc.gpsimd)
-        load_scales(t_scales, 0, S)
+        load_vector(nc.scalar, a2_bf, a2)
+        load_vector(nc.scalar, b2_bf, b2)
+        nc.gpsimd.dma_start(out=t_codes[:].bitcast(I32), in_=t_words[0].bitcast(I32))
+        load_vector(nc.gpsimd, ls_bf, ls)
+        load_scales(t_sc, t_scales)
         load_x(1, 0, 4)
-        nc.sync.dma_start(out=ww[:].bitcast(I32), in_=w_words[0].bitcast(I32))
-        load_scales(w_scales, S, F)
+        nc.sync.dma_start(out=w_codes[:].bitcast(I32), in_=w_words[0].bitcast(I32))
+        load_scales(w_sc, w_scales)
         load_x(2, 0, 4)
         load_x(3, 0, 4)
+        warm = const.tile([P, 1], F32, name="warm")
+        nc.vector.memset(warm[:], 0.0)
         nc.scalar.activation(warm[:], warm[:], ACT.Gelu)
-        nc.vector.tensor_copy(out=gtf[:], in_=gtt[:])
-        nc.vector.tensor_copy(out=a2f[:], in_=a2t[:])
-        nc.vector.tensor_copy(out=b2f[:], in_=b2t[:])
+        nc.vector.tensor_copy(out=gt_f32[:], in_=gt_bf[:])
+        nc.vector.tensor_copy(out=a2_f32[:], in_=a2_bf[:])
+        nc.vector.tensor_copy(out=b2_f32[:], in_=b2_bf[:])
 
-        live = {}
+        tiles = {}
 
-        def get(pool, shape, dtype, kind, b):
-            if (kind, b) not in live:
-                live[kind, b] = pool.tile(
-                    shape, dtype, name=f"{kind}_{b}", tag=kind, align_bytes=64
+        def tile(pool, shape, dtype, kind, index):
+            if (kind, index) not in tiles:
+                tiles[kind, index] = pool.tile(
+                    shape, dtype, name=f"{kind}_{index}", tag=kind, align_bytes=64
                 )
-            return live[kind, b]
+            return tiles[kind, index]
+
+        def gated(b):
+            return tile(pair, [P, 4, D], BF16, "gated", b)
+
+        def n_woven(b):
+            return tile(three, [P, 4, P, 4], BF16, "n_woven", b)
+
+        def n_codes(b):
+            return tile(three, [P, D], U32, "n_codes", b), tile(three, [P, D], U8, "n_scales", b)
+
+        def y_tile(b):
+            return tile(three, [P, 4, S], F32, "y", b)
+
+        def u_codes(b):
+            return tile(pair, [P, S], U32, "u_codes", b), tile(pair, [P, S], U8, "u_scales", b)
 
         def gate(b, engine):
-            g = get(two, [P, 4, D], BF16, "gated", b)
-            for j in range(4):
-                if j < SCALAR_GATES[b]:
-                    if engine == "scalar":
-                        nc.scalar.activation(
-                            g[:, j, :], xs[b][:, j, :], ACT.Copy, scale=gtf[:, j : j + 1]
-                        )
-                elif engine == "vector":
+            if engine == "scalar":
+                for j in range(SCALAR_GATES[b]):
+                    nc.scalar.activation(
+                        gated(b)[:, j, :], xs[b][:, j, :], ACT.Copy, scale=gt_f32[:, j : j + 1]
+                    )
+            else:
+                for j in range(SCALAR_GATES[b], 4):
                     nc.vector.tensor_scalar(
-                    g[:, j, :], xs[b][:, j, :], gtt[:, j : j + 1], None, op0=ALU.mult
-                )
+                        gated(b)[:, j, :], xs[b][:, j, :], gt_bf[:, j : j + 1], None, op0=ALU.mult
+                    )
 
-        def weave_n(b, m0, m1, engine):
-            g = get(two, [P, 4, D], BF16, "gated", b)
-            ni = get(two, [P, 4, P, 4], BF16, "nwoven", b)
-            copy = nc.vector.tensor_copy if engine == "vector" else nc.scalar.copy
+        def weave_n(copy, b, m0, m1):
             copy(
-                out=ni[:, :, m0:m1, :].rearrange("p t m j -> p m j t"),
-                in_=g[:].rearrange("p j (m t) -> p m j t", t=4)[:, m0:m1],
+                out=n_woven(b)[:, :, m0:m1, :].rearrange("p t m j -> p m j t"),
+                in_=gated(b)[:].rearrange("p j (m t) -> p m j t", t=4)[:, m0:m1],
             )
 
-        def quant_n(b, t0, t1):
-            ni = get(two, [P, 4, P, 4], BF16, "nwoven", b)
-            nq = get(two, [P, D], U32, "ncodes", b)
-            ns = get(two, [P, D], U8, "nscales", b)
-            nc.vector.quantize_mx(
-                out=nq[:, P * t0 : P * t1].bitcast(FP8X4),
-                scales=ns[:, P * t0 : P * t1],
-                in_=ni[:, t0:t1].rearrange("p t m j -> p (t m j)"),
-            )
+        def quant_n(b):
+            codes, sc = n_codes(b)
+            for half in range(2):
+                cols = slice(2 * P * half, 2 * P * (half + 1))
+                nc.vector.quantize_mx(
+                    out=codes[:, cols].bitcast(FP8X4),
+                    scales=sc[:, cols],
+                    in_=n_woven(b)[:, 2 * half : 2 * half + 2].rearrange("p t m j -> p (t m j)"),
+                )
 
         def turn_x(b, u, pool, tag):
             words = xs[b][:].rearrange("p j d -> p (j d)").bitcast(F32)
-            bank = pool.tile([P, 4, P], F32, name=f"xt{b}_{u}", tag=tag)
-            live["xt", b, u] = bank
+            bank = pool.tile([P, 4, P], F32, name=f"x_turned_{b}_{u}", tag=tag)
+            tiles["x_turned", b, u] = bank
             for j in range(4):
                 nc.tensor.transpose(
                     bank[:, j, :], words[:, 256 * j + u : 256 * (j + 1) : 2], ident[:]
                 )
 
-        def affine(b, u, i0=0, n=S):
-            y = get(ypool, [P, 4, S], F32, "y", b)
-            view = live["xt", b, u][:].rearrange("p j q -> p (j q)").bitcast(BF16)
-            view = view.rearrange("p (j q e) -> p q j e", j=4, e=2)
+        def affine(b, u):
+            halves = tiles["x_turned", b, u][:].rearrange("p j q -> p (j q)").bitcast(BF16)
+            halves = halves.rearrange("p (j q e) -> p q j e", j=4, e=2)
             for e in range(2):
                 t = 2 * u + e
                 nc.scalar.activation(
-                    y[:, t, i0 : i0 + n].rearrange("p (q j) -> p q j", j=4),
-                    view[:, i0 // 4 : (i0 + n) // 4, :, e],
+                    y_tile(b)[:, t, :].rearrange("p (q j) -> p q j", j=4),
+                    halves[:, :, :, e],
                     ACT.Identity,
-                    bias=b2f[:, t : t + 1],
-                    scale=a2f[:, t : t + 1],
+                    bias=b2_f32[:, t : t + 1],
+                    scale=a2_f32[:, t : t + 1],
                 )
 
-        def mix_mm(b, i0, n, chans):
-            nq = get(two, [P, D], U32, "ncodes", b)
-            ns = get(two, [P, D], U8, "nscales", b)
-            per = 512 // n
-            for t in chans:
-                if t % per == 0:
-                    bank = mix.tile([P, per, n], F32, name=f"m{b}_{i0}_{t}", tag="m")
-                live["m", b, i0, t] = bank[:, t % per, :]
+        def mix(b, slots_t):
+            codes, sc = n_codes(b)
+            for t in slots_t:
                 cols = slice(P * t, P * (t + 1))
+                bank = mix_banks.tile([P, S], F32, name=f"m_{b}_{t}", tag="m")
                 nc.tensor.matmul_mx(
-                    out=bank[:, t % per, :],
-                    lhsT=nq[:, cols].bitcast(FP8X4),
-                    lhsT_scale=ns[:, cols],
-                    rhs=tw[:, 2 * i0 : 2 * (i0 + n)].bitcast(FP4X4),
-                    rhs_scale=ts[:, i0 : i0 + n],
+                    out=bank[:],
+                    lhsT=codes[:, cols].bitcast(FP8X4),
+                    lhsT_scale=sc[:, cols],
+                    rhs=t_codes[:].bitcast(FP4X4),
+                    rhs_scale=t_sc,
                     start=True,
                     stop=True,
                 )
-
-        def residual(b, i0, n, chans=range(4)):
-            y = get(ypool, [P, 4, S], F32, "y", b)
-            ub = get(two, [P, 4, S], BF16, "u", b)
-            for t in chans:
                 nc.vector.scalar_tensor_tensor(
-                    ub[:, t, i0 : i0 + n],
-                    live["m", b, i0, t],
-                    la[:, t : t + 1],
-                    y[:, t, i0 : i0 + n],
+                    tile(pair, [P, 4, S], BF16, "u", b)[:, t, :],
+                    bank[:],
+                    ls_a2[:, t : t + 1],
+                    y_tile(b)[:, t, :],
                     op0=ALU.mult,
                     op1=ALU.add,
                 )
 
-        def weave_u(b, i0, n):
-            ub = get(two, [P, 4, S], BF16, "u", b)
-            ui = get(two, [P, S, 4], BF16, "uwoven", b)
+        def weave_u(b):
             nc.vector.tensor_copy(
-                out=ui[:, i0 : i0 + n, :].rearrange("p (c i) t -> p c t i", i=4),
-                in_=ub[:, :, i0 : i0 + n].rearrange("p t (c i) -> p c t i", i=4),
+                out=tile(pair, [P, S, 4], BF16, "u_woven", b)[:].rearrange("p (c i) t -> p c t i", i=4),
+                in_=tiles["u", b][:].rearrange("p t (c i) -> p c t i", i=4),
             )
 
-        def quant_u(b, i0, n):
-            ui = get(two, [P, S, 4], BF16, "uwoven", b)
-            uq = get(two, [P, S], U32, "ucodes", b)
-            us = get(two, [P, S], U8, "uscales", b)
+        def quant_u(b):
+            codes, sc = u_codes(b)
             nc.vector.quantize_mx(
-                out=uq[:, i0 : i0 + n].bitcast(FP8X4),
-                scales=us[:, i0 : i0 + n],
-                in_=ui[:, i0 : i0 + n, :].rearrange("p i t -> p (i t)"),
+                out=codes[:].bitcast(FP8X4),
+                scales=sc[:],
+                in_=tiles["u_woven", b][:].rearrange("p i t -> p (i t)"),
             )
 
         def project(k):
-            b, tb = divmod(k, 4)
-            uq = get(two, [P, S], U32, "ucodes", b)
-            us = get(two, [P, S], U8, "uscales", b)
-            o = get(opool, [P, F], F32, "o", k)
-            toks = slice(P * tb, P * (tb + 1))
-            for h in range(2):
-                cols = slice(512 * h, 512 * (h + 1))
-                bank = wide.tile([P, 512], F32, name=f"h{k}_{h}", tag="w")
+            b, part = divmod(k, 4)
+            codes, sc = u_codes(b)
+            toks = slice(P * part, P * (part + 1))
+            result = tile(results, [P, F], F32, "result", k)
+            for half in range(2):
+                cols = slice(BANK * half, BANK * (half + 1))
+                bank = wide_banks.tile([P, BANK], F32, name=f"h_{k}_{half}", tag="w")
                 nc.tensor.matmul_mx(
                     out=bank[:],
-                    lhsT=uq[:, toks].bitcast(FP8X4),
-                    lhsT_scale=us[:, toks],
-                    rhs=ww[:, 1024 * h : 1024 * (h + 1)].bitcast(FP4X4),
-                    rhs_scale=ws[:, cols],
+                    lhsT=codes[:, toks].bitcast(FP8X4),
+                    lhsT_scale=sc[:, toks],
+                    rhs=w_codes[:, 2 * BANK * half : 2 * BANK * (half + 1)].bitcast(FP4X4),
+                    rhs_scale=w_sc[:, cols],
                     start=True,
                     stop=True,
                 )
-                nc.scalar.activation(o[:, cols], bank[:], ACT.Gelu)
-            nc.sync.dma_start(out=out_0[b, toks, :], in_=o[:])
+                nc.scalar.activation(result[:, cols], bank[:], ACT.Gelu)
+            nc.sync.dma_start(out=out_0[b, toks, :], in_=result[:])
 
-        def round_o(k):
-            ob = get(qpool, [P, F], BF16, "orounded", k)
-            nc.vector.tensor_copy(out=ob[:], in_=live["o", k][:])
+        def round_result(k):
+            rounded = tile(rounded_pool, [P, F], BF16, "rounded", k)
+            nc.vector.tensor_copy(out=rounded[:], in_=tiles["result", k][:])
 
-        def turn_o(k):
-            words = live["orounded", k][:].bitcast(F32)
-            bank = wide.tile([P, 2, 2, P], F32, name=f"ot{k}", tag="w")
-            live["ot", k] = bank
+        def turn_result(k):
+            words = tiles["rounded", k][:].bitcast(F32)
+            bank = wide_banks.tile([P, 2, 2, P], F32, name=f"turned_{k}", tag="w")
+            tiles["turned", k] = bank
             for g in range(2):
                 for u in range(2):
                     nc.tensor.transpose(
                         bank[:, g, u, :], words[:, 256 * g + u : 256 * (g + 1) : 2], ident[:]
                     )
 
-        def copy_o(k):
-            b, tb = divmod(k, 4)
-            pt = get(ppool, [P, 2, S, 4], BF16, "pwoven", b)
+        def weave_result(k):
+            b, part = divmod(k, 4)
+            woven = tile(three, [P, 2, S, 4], BF16, "woven", b)
             copy = nc.vector.tensor_copy if k in VECTOR_COPIES else nc.scalar.copy
-            for g in range(2):
-                dst = pt[:, g, P * tb : P * (tb + 1), :].rearrange("p r t -> p (r t)")
-                copy(
-                    out=dst.bitcast(F32).rearrange("p (r u) -> p r u", u=2),
-                    in_=live["ot", k][:, g].rearrange("p u r -> p r u"),
-                )
+            dst = woven[:, :, P * part : P * (part + 1), :].rearrange("p g r t -> p g (r t)")
+            copy(
+                out=dst.bitcast(F32).rearrange("p g (r u) -> p g r u", u=2),
+                in_=tiles["turned", k][:].rearrange("p g u r -> p g r u"),
+            )
 
         def planes(b, g, i0, n):
-            pt = live["pwoven", b]
-            pc = get(two, [P, 2, 2 * S], U8, "pscales", b // 2)
-            pq = get(qpool, [P, S], U32, "pcodes", (b, g, i0))
-            c0 = b % 2 * S + i0
-            m0 = b * S + i0
+            sc = tile(pair, [P, 2, 2 * S], U8, "plane_scales", b // 2)
+            codes = tile(codes_pool, [P, S], U32, "plane_codes", (b, g, i0))
+            s0 = S * (b % 2) + i0
+            m0 = S * b + i0
             nc.vector.quantize_mx(
-                out=pq[:, 0:n].bitcast(FP8X4),
-                scales=pc[:, g, c0 : c0 + n],
-                in_=pt[:, g, i0 : i0 + n, :].rearrange("p i t -> p (i t)"),
+                out=codes[:, 0:n].bitcast(FP8X4),
+                scales=sc[:, g, s0 : s0 + n],
+                in_=tiles["woven", b][:, g, i0 : i0 + n, :].rearrange("p i t -> p (i t)"),
             )
             nc.sync.dma_start(
                 out=out_1[g, :, m0 : m0 + n, :].rearrange("p m t -> p (m t)").bitcast(I32),
-                in_=pq[:, 0:n].bitcast(I32),
+                in_=codes[:, 0:n].bitcast(I32),
             )
 
-        def store_scales(pair):
-            m0 = 2 * S * pair
+        def store_scales(half):
+            m0 = 2 * S * half
             for q in range(4):
+                rows = out_2[:, 4 * q : 4 * q + 4, m0 : m0 + 2 * S].rearrange("g q m -> q g m")
                 nc.sync.dma_start(
-                    out=out_2[:, 4 * q : 4 * q + 4, m0 : m0 + 2 * S]
-                    .rearrange("g q m -> q g m")
-                    .bitcast(I32),
-                    in_=live["pscales", pair][32 * q : 32 * q + 4, :, :].bitcast(I32),
+                    out=rows.bitcast(I32),
+                    in_=tiles["plane_scales", half][32 * q : 32 * q + 4, :, :].bitcast(I32),
                 )
 
-        turn_x(0, 0, wide, "w")
-        turn_x(0, 1, wide, "w")
+        turn_x(0, 0, wide_banks, "w")
+        turn_x(0, 1, wide_banks, "w")
         gate(0, "vector")
-        weave_n(0, 0, 96, "vector")
-        weave_n(0, 96, 128, "scalar")
-        quant_n(0, 0, 2)
-        quant_n(0, 2, 4)
-        nc.vector.tensor_tensor(la[:], lst[:], a2t[:], op=ALU.mult)
-        for i0, n in ((0, 128), (128, 384)):
-            for u in range(2):
-                affine(0, u, i0, n)
+        weave_n(nc.vector.tensor_copy, 0, 0, VECTOR_WEAVE)
+        weave_n(nc.scalar.copy, 0, VECTOR_WEAVE, P)
+        quant_n(0)
+        affine(0, 0)
+        affine(0, 1)
         gate(1, "scalar")
-        mix_mm(0, 0, 128, range(4))
-        mix_mm(0, 128, 128, range(4))
-        residual(0, 0, 128)
+        nc.vector.tensor_tensor(ls_a2[:], ls_bf[:], a2_bf[:], op=ALU.mult)
+        mix(0, range(4))
         gate(1, "vector")
-        weave_u(0, 0, 128)
-        residual(0, 128, 128)
-        quant_u(0, 0, 128)
-        mix_mm(0, 256, 256, range(4))
-        weave_u(0, 128, 128)
-        residual(0, 256, 256, (0, 1))
-        quant_u(0, 128, 128)
-        residual(0, 256, 256, (2, 3))
-        weave_u(0, 256, 256)
-        weave_n(1, 0, 128, "vector")
-        quant_u(0, 256, 256)
-        quant_n(1, 0, 2)
-        quant_n(1, 2, 4)
+        weave_u(0)
+        weave_n(nc.vector.tensor_copy, 1, 0, P)
+        quant_u(0)
+        quant_n(1)
 
         for k in range(N_TILES):
-            if k >= 2:
-                round_o(k - 2)
-            if k == 0:
-                for c in (2, 3):
-                    gate(c, "scalar")
-                for c in (2, 3):
-                    weave_n(c, 0, 128, "vector")
-            for c in range(1, B):
-                if AFFINE_SLOTS[c] == k:
-                    for u in range(2):
-                        turn_x(c, u, mix, "m")
-                        affine(c, u)
-            project(k)
-            if k >= 4:
-                turn_o(k - 4)
-            for c in range(1, B):
-                if WEAVE_SLOTS[c] == k - 1:
-                    quant_u(c, 0, 512)
-            if k >= 4:
-                copy_o(k - 4)
-            if k in PLANE_SLOTS:
-                planes(*PLANE_SLOTS[k], 0, 512)
-                if PLANE_SLOTS[k] == (1, 1):
-                    store_scales(0)
-            for c in range(1, B):
-                chans = [t for t in range(4) if MIX_SLOTS[c][t] == k]
-                mix_mm(c, 0, 512, chans)
-                residual(c, 0, 512, chans)
-            if k < 2:
-                quant_n(k + 2, 0, 2)
-                quant_n(k + 2, 2, 4)
-            for c in range(1, B):
-                if WEAVE_SLOTS[c] == k:
-                    weave_u(c, 0, 512)
 
-        round_o(14)
-        turn_o(12)
-        turn_o(13)
-        copy_o(12)
-        round_o(15)
-        turn_o(14)
-        copy_o(13)
-        turn_o(15)
+            def due(step):
+                return [b for b in STEPS if STEPS[b].get(step) == k]
+
+            turned = [i for i in range(N_TILES) if round_slot(i) == k - 1]
+            for i in turned:
+                turn_result(i)
+            for b in due("weave_u"):
+                weave_u(b)
+            for b in due("gate_scalar"):
+                gate(b, "scalar")
+            for i in range(N_TILES):
+                if round_slot(i) == k:
+                    round_result(i)
+            for b, g in PLANE_SLOTS.get(k, ()):
+                planes(b, g, 0, S)
+            if k == max(PLANE_SLOTS):
+                store_scales(0)
+            for b in due("quant_n"):
+                quant_n(b)
+            for b in due("quant_u"):
+                quant_u(b)
+            for b in due("gate_vector"):
+                gate(b, "vector")
+            for i in turned:
+                weave_result(i)
+            for u in range(2):
+                for b in STEPS:
+                    if STEPS[b]["affine"][u] == k:
+                        turn_x(b, u, mix_banks, "m")
+                        affine(b, u)
+            for b in due("weave_n"):
+                weave_n(nc.vector.tensor_copy, b, 0, P)
+            for b in STEPS:
+                mix(b, [t for t in range(4) if STEPS[b]["mix"][t] == k])
+            project(k)
+
+        turn_result(12)
+        round_result(13)
+        turn_result(13)
+        round_result(14)
+        turn_result(14)
+        weave_result(12)
+        round_result(15)
+        turn_result(15)
+        weave_result(13)
         for g in range(2):
-            planes(3, g, 0, 256)
-        copy_o(14)
-        copy_o(15)
+            planes(3, g, 0, S // 2)
+        weave_result(14)
+        weave_result(15)
         for g in range(2):
-            planes(2, g, 0, 512)
+            planes(2, g, 0, S)
         for g in range(2):
-            planes(3, g, 256, 256)
+            planes(3, g, S // 2, S // 2)
         store_scales(1)

from contextlib import ExitStack

import concourse.mybir as mybir
from concourse.masks import make_identity

B, S, D, F = 4, 512, 512, 1024
FLOPS = 2 * B * S * S * D + 2 * B * S * D * F

F32 = mybir.dt.float32
BF16 = mybir.dt.bfloat16
I32 = mybir.dt.int32
U32 = mybir.dt.uint32
U8 = mybir.dt.uint8
FP8X4 = mybir.dt.float8_e4m3fn_x4
FP4X4 = mybir.dt.float4_e2m1fn_x4
ACT = mybir.ActivationFunctionType
ALU = mybir.AluOpType

P = 128
BANK = 512
N_TILES = B * S // P

STEPS = {
    1: dict(affine=(0, 0), mix=(0, 1, 1, 1), weave_u=3, quant_u=4),
    2: dict(gate_scalar=0, weave_n=0, quant_n=1, affine=(0, 0), mix=(2, 3, 4, 4), weave_u=7, quant_u=7),
    3: dict(
        gate_scalar=1, gate_vector=0, weave_n=6, quant_n=7, affine=(4, 7), mix=(8, 8, 9, 9), weave_u=11, quant_u=11
    ),
}
SCALAR_GATES = (0, 2, 4, 3)
VECTOR_WEAVE = 96
VECTOR_COPIES = (4, 9, 12)
PLANE_SLOTS = {12: ((0, 0),), 13: ((0, 1),), 14: ((1, 0), (1, 1))}


def round_slot(k):
    return max(k + 3, 8 + 5 * k // 8)


def tile_resmlpcrosspatchintochannelexpansion_x2_kernel(
    tc, x, gt, t_words, t_scales, ls, a2, b2, w_words, w_scales, out_0, out_1, out_2
):
    nc = tc.nc
    with ExitStack() as ctx:
        const = ctx.enter_context(tc.tile_pool(name="const", bufs=1))
        pair = ctx.enter_context(tc.tile_pool(name="pair", bufs=2))
        three = ctx.enter_context(tc.tile_pool(name="three", bufs=3))
        results = ctx.enter_context(tc.tile_pool(name="results", bufs=12))
        rounded_pool = ctx.enter_context(tc.tile_pool(name="rounded", bufs=4))
        codes_pool = ctx.enter_context(tc.tile_pool(name="codes", bufs=6))
        mix_banks = ctx.enter_context(tc.psum_pool(name="mix_banks", bufs=3))
        wide_banks = ctx.enter_context(tc.psum_pool(name="wide_banks", bufs=5))
        ctx.enter_context(tc.manual_schedule())

        xs = []
        for b in range(B):
            xb = const.tile([P, 4, D], BF16, name=f"x{b}", align_bytes=64)
            xs.append(xb)
        gt_bf = const.tile([P, 4], BF16, name="gt_bf")
        ls_bf = const.tile([P, 4], BF16, name="ls_bf")
        a2_bf = const.tile([P, 4], BF16, name="a2_bf")
        b2_bf = const.tile([P, 4], BF16, name="b2_bf")
        a2_f32 = const.tile([P, 4], F32, name="a2_f32")
        b2_f32 = const.tile([P, 4], F32, name="b2_f32")
        ls_a2 = const.tile([P, 4], F32, name="ls_a2")
        gt_f32 = const.tile([P, 4], F32, name="gt_f32")
        t_codes = const.tile([P, 2 * S], U8, name="t_codes", align_bytes=64)
        w_codes = const.tile([P, 2 * F], U8, name="w_codes", align_bytes=64)
        scales = const.tile([P, S + F], U8, name="scales", align_bytes=64)
        ident = const.tile([P, P], F32, name="ident", align_bytes=64)
        t_sc = scales[:, 0:S]
        w_sc = scales[:, S : S + F]

        def load_x(b, j0, j1):
            nc.sync.dma_start(
                out=xs[b][:, j0:j1, :],
                in_=x[b].rearrange("(p j) d -> p j d", j=4)[:, j0:j1, :],
            )

        def load_vector(engine, dst, src):
            engine.dma_start(out=dst[:], in_=src.rearrange("(p t) -> p t", t=4))

        def load_scales(dst, src):
            for q in range(4):
                nc.sync.dma_start(
                    out=dst[32 * q : 32 * q + 4, :].bitcast(I32),
                    in_=src[0, 4 * q : 4 * q + 4, :].bitcast(I32),
                )

        nc.vector.memset(scales[:].bitcast(I32), 0)
        make_identity(nc, ident[:])
        load_vector(nc.scalar, gt_bf, gt)
        load_x(0, 0, 2)
        load_x(0, 2, 4)
        load_vector(nc.scalar, a2_bf, a2)
        load_vector(nc.scalar, b2_bf, b2)
        nc.gpsimd.dma_start(out=t_codes[:].bitcast(I32), in_=t_words[0].bitcast(I32))
        load_vector(nc.gpsimd, ls_bf, ls)
        load_scales(t_sc, t_scales)
        load_x(1, 0, 4)
        nc.sync.dma_start(out=w_codes[:].bitcast(I32), in_=w_words[0].bitcast(I32))
        load_scales(w_sc, w_scales)
        load_x(2, 0, 4)
        load_x(3, 0, 4)
        warm = const.tile([P, 1], F32, name="warm")
        nc.vector.memset(warm[:], 0.0)
        nc.scalar.activation(warm[:], warm[:], ACT.Gelu)
        nc.vector.tensor_copy(out=gt_f32[:], in_=gt_bf[:])
        nc.vector.tensor_copy(out=a2_f32[:], in_=a2_bf[:])
        nc.vector.tensor_copy(out=b2_f32[:], in_=b2_bf[:])

        tiles = {}

        def tile(pool, shape, dtype, kind, index):
            if (kind, index) not in tiles:
                tiles[kind, index] = pool.tile(
                    shape, dtype, name=f"{kind}_{index}", tag=kind, align_bytes=64
                )
            return tiles[kind, index]

        def gated(b):
            return tile(pair, [P, 4, D], BF16, "gated", b)

        def n_woven(b):
            return tile(three, [P, 4, P, 4], BF16, "n_woven", b)

        def n_codes(b):
            return tile(three, [P, D], U32, "n_codes", b), tile(three, [P, D], U8, "n_scales", b)

        def y_tile(b):
            return tile(three, [P, 4, S], F32, "y", b)

        def u_codes(b):
            return tile(pair, [P, S], U32, "u_codes", b), tile(pair, [P, S], U8, "u_scales", b)

        def gate(b, engine):
            if engine == "scalar":
                for j in range(SCALAR_GATES[b]):
                    nc.scalar.activation(
                        gated(b)[:, j, :], xs[b][:, j, :], ACT.Copy, scale=gt_f32[:, j : j + 1]
                    )
            else:
                for j in range(SCALAR_GATES[b], 4):
                    nc.vector.tensor_scalar(
                        gated(b)[:, j, :], xs[b][:, j, :], gt_bf[:, j : j + 1], None, op0=ALU.mult
                    )

        def weave_n(copy, b, m0, m1):
            copy(
                out=n_woven(b)[:, :, m0:m1, :].rearrange("p t m j -> p m j t"),
                in_=gated(b)[:].rearrange("p j (m t) -> p m j t", t=4)[:, m0:m1],
            )

        def quant_n(b):
            codes, sc = n_codes(b)
            for half in range(2):
                cols = slice(2 * P * half, 2 * P * (half + 1))
                nc.vector.quantize_mx(
                    out=codes[:, cols].bitcast(FP8X4),
                    scales=sc[:, cols],
                    in_=n_woven(b)[:, 2 * half : 2 * half + 2].rearrange("p t m j -> p (t m j)"),
                )

        def turn_x(b, u, pool, tag):
            words = xs[b][:].rearrange("p j d -> p (j d)").bitcast(F32)
            bank = pool.tile([P, 4, P], F32, name=f"x_turned_{b}_{u}", tag=tag)
            tiles["x_turned", b, u] = bank
            for j in range(4):
                nc.tensor.transpose(
                    bank[:, j, :], words[:, 256 * j + u : 256 * (j + 1) : 2], ident[:]
                )

        def affine(b, u):
            halves = tiles["x_turned", b, u][:].rearrange("p j q -> p (j q)").bitcast(BF16)
            halves = halves.rearrange("p (j q e) -> p q j e", j=4, e=2)
            for e in range(2):
                t = 2 * u + e
                nc.scalar.activation(
                    y_tile(b)[:, t, :].rearrange("p (q j) -> p q j", j=4),
                    halves[:, :, :, e],
                    ACT.Identity,
                    bias=b2_f32[:, t : t + 1],
                    scale=a2_f32[:, t : t + 1],
                )

        def mix(b, slots_t):
            codes, sc = n_codes(b)
            for t in slots_t:
                cols = slice(P * t, P * (t + 1))
                bank = mix_banks.tile([P, S], F32, name=f"m_{b}_{t}", tag="m")
                nc.tensor.matmul_mx(
                    out=bank[:],
                    lhsT=codes[:, cols].bitcast(FP8X4),
                    lhsT_scale=sc[:, cols],
                    rhs=t_codes[:].bitcast(FP4X4),
                    rhs_scale=t_sc,
                    start=True,
                    stop=True,
                )
                nc.vector.scalar_tensor_tensor(
                    tile(pair, [P, 4, S], BF16, "u", b)[:, t, :],
                    bank[:],
                    ls_a2[:, t : t + 1],
                    y_tile(b)[:, t, :],
                    op0=ALU.mult,
                    op1=ALU.add,
                )

        def weave_u(b):
            nc.vector.tensor_copy(
                out=tile(pair, [P, S, 4], BF16, "u_woven", b)[:].rearrange("p (c i) t -> p c t i", i=4),
                in_=tiles["u", b][:].rearrange("p t (c i) -> p c t i", i=4),
            )

        def quant_u(b):
            codes, sc = u_codes(b)
            nc.vector.quantize_mx(
                out=codes[:].bitcast(FP8X4),
                scales=sc[:],
                in_=tiles["u_woven", b][:].rearrange("p i t -> p (i t)"),
            )

        def project(k):
            b, part = divmod(k, 4)
            codes, sc = u_codes(b)
            toks = slice(P * part, P * (part + 1))
            result = tile(results, [P, F], F32, "result", k)
            for half in range(2):
                cols = slice(BANK * half, BANK * (half + 1))
                bank = wide_banks.tile([P, BANK], F32, name=f"h_{k}_{half}", tag="w")
                nc.tensor.matmul_mx(
                    out=bank[:],
                    lhsT=codes[:, toks].bitcast(FP8X4),
                    lhsT_scale=sc[:, toks],
                    rhs=w_codes[:, 2 * BANK * half : 2 * BANK * (half + 1)].bitcast(FP4X4),
                    rhs_scale=w_sc[:, cols],
                    start=True,
                    stop=True,
                )
                nc.scalar.activation(result[:, cols], bank[:], ACT.Gelu)
            nc.sync.dma_start(out=out_0[b, toks, :], in_=result[:])

        def round_result(k):
            rounded = tile(rounded_pool, [P, F], BF16, "rounded", k)
            nc.vector.tensor_copy(out=rounded[:], in_=tiles["result", k][:])

        def turn_result(k):
            words = tiles["rounded", k][:].bitcast(F32)
            bank = wide_banks.tile([P, 2, 2, P], F32, name=f"turned_{k}", tag="w")
            tiles["turned", k] = bank
            for g in range(2):
                for u in range(2):
                    nc.tensor.transpose(
                        bank[:, g, u, :], words[:, 256 * g + u : 256 * (g + 1) : 2], ident[:]
                    )

        def weave_result(k):
            b, part = divmod(k, 4)
            woven = tile(three, [P, 2, S, 4], BF16, "woven", b)
            copy = nc.vector.tensor_copy if k in VECTOR_COPIES else nc.scalar.copy
            dst = woven[:, :, P * part : P * (part + 1), :].rearrange("p g r t -> p g (r t)")
            copy(
                out=dst.bitcast(F32).rearrange("p g (r u) -> p g r u", u=2),
                in_=tiles["turned", k][:].rearrange("p g u r -> p g r u"),
            )

        def planes(b, g, i0, n):
            sc = tile(pair, [P, 2, 2 * S], U8, "plane_scales", b // 2)
            codes = tile(codes_pool, [P, S], U32, "plane_codes", (b, g, i0))
            s0 = S * (b % 2) + i0
            m0 = S * b + i0
            nc.vector.quantize_mx(
                out=codes[:, 0:n].bitcast(FP8X4),
                scales=sc[:, g, s0 : s0 + n],
                in_=tiles["woven", b][:, g, i0 : i0 + n, :].rearrange("p i t -> p (i t)"),
            )
            nc.sync.dma_start(
                out=out_1[g, :, m0 : m0 + n, :].rearrange("p m t -> p (m t)").bitcast(I32),
                in_=codes[:, 0:n].bitcast(I32),
            )

        def store_scales(half):
            m0 = 2 * S * half
            for q in range(4):
                rows = out_2[:, 4 * q : 4 * q + 4, m0 : m0 + 2 * S].rearrange("g q m -> q g m")
                nc.sync.dma_start(
                    out=rows.bitcast(I32),
                    in_=tiles["plane_scales", half][32 * q : 32 * q + 4, :, :].bitcast(I32),
                )

        turn_x(0, 0, wide_banks, "w")
        turn_x(0, 1, wide_banks, "w")
        gate(0, "vector")
        weave_n(nc.vector.tensor_copy, 0, 0, VECTOR_WEAVE)
        weave_n(nc.scalar.copy, 0, VECTOR_WEAVE, P)
        quant_n(0)
        affine(0, 0)
        affine(0, 1)
        gate(1, "scalar")
        nc.vector.tensor_tensor(ls_a2[:], ls_bf[:], a2_bf[:], op=ALU.mult)
        mix(0, range(4))
        gate(1, "vector")
        weave_u(0)
        weave_n(nc.vector.tensor_copy, 1, 0, P)
        quant_u(0)
        quant_n(1)

        for k in range(N_TILES):

            def due(step):
                return [b for b in STEPS if STEPS[b].get(step) == k]

            turned = [i for i in range(N_TILES) if round_slot(i) == k - 1]
            for i in turned:
                turn_result(i)
            for b in due("weave_u"):
                weave_u(b)
            for b in due("gate_scalar"):
                gate(b, "scalar")
            for i in range(N_TILES):
                if round_slot(i) == k:
                    round_result(i)
            for b, g in PLANE_SLOTS.get(k, ()):
                planes(b, g, 0, S)
            if k == max(PLANE_SLOTS):
                store_scales(0)
            for b in due("quant_n"):
                quant_n(b)
            for b in due("quant_u"):
                quant_u(b)
            for b in due("gate_vector"):
                gate(b, "vector")
            for i in turned:
                weave_result(i)
            for u in range(2):
                for b in STEPS:
                    if STEPS[b]["affine"][u] == k:
                        turn_x(b, u, mix_banks, "m")
                        affine(b, u)
            for b in due("weave_n"):
                weave_n(nc.vector.tensor_copy, b, 0, P)
            for b in STEPS:
                mix(b, [t for t in range(4) if STEPS[b]["mix"][t] == k])
            project(k)

        turn_result(12)
        round_result(13)
        turn_result(13)
        round_result(14)
        turn_result(14)
        weave_result(12)
        round_result(15)
        turn_result(15)
        weave_result(13)
        for g in range(2):
            planes(3, g, 0, S // 2)
        weave_result(14)
        weave_result(15)
        for g in range(2):
            planes(2, g, 0, S)
        for g in range(2):
            planes(3, g, S // 2, S // 2)
        store_scales(1)
